import numpy as np
import ml_dtypes


def mxq(x, axis, fmt="e4m3"):
    dtype, down = {"e4m3": (ml_dtypes.float8_e4m3fn, 7), "e5m2": (ml_dtypes.float8_e5m2, 14)}[fmt]
    v = np.moveaxis(np.asarray(x, np.float32).astype(ml_dtypes.bfloat16).astype(np.float64), axis, -1)
    blocks = v.reshape(v.shape[:-1] + (-1, 32))
    amax = np.abs(blocks).max(-1, keepdims=True)
    byte = np.maximum(np.where(amax > 0, np.frexp(amax)[1] - 1 + 127, 0) - down, 1)
    scale = np.exp2(byte - 127.0)
    codes = (blocks / scale).astype(np.float32).astype(dtype).astype(np.float64)
    return np.moveaxis((codes * scale).reshape(v.shape), -1, axis)


WIDE = False


def mx_kscale(k):
    if not WIDE:
        return np.ones(k)
    levels = np.array([10, -10, 5, -5, 0])
    if k % 512:
        return np.exp2(np.random.permutation(np.resize(levels, k // 32))).repeat(32)
    a = np.empty((k // 512, 16))
    for p in range(k // 512):
        a[p, :8] = np.random.permutation(np.resize(levels, 8))
        for g in range(8):
            far = levels[np.abs(levels - a[p, g]) >= 10]
            a[p, g + 8] = far[np.random.randint(len(far))]
    return np.exp2(a.ravel()).repeat(32)


def f64(x):
    return np.asarray(x).astype(np.float64)


def striped(idx):
    return np.tile(idx.reshape(-1, 16).T, (8, 1)).astype(np.uint16)


def unstriped(offs):
    return offs[:16].T.reshape(-1).astype(np.int64)


E2M1 = np.array([0.0, 0.5, 1.0, 1.5, 2.0, 3.0, 4.0, 6.0, -0.0, -0.5, -1.0, -1.5, -2.0, -3.0, -4.0, -6.0])


def pack_fp4(w):
    k, n = w.shape
    w = f64(np.asarray(w, np.float32).astype(ml_dtypes.bfloat16)).reshape(k // 32, 32, n)
    amax = np.abs(w).max(1)
    mant, ex = np.frexp(amax / 6.0)
    byte = np.clip(np.where(amax > 0, np.where(mant > 0.5, ex, ex - 1) + 127, 1), 1, 254)
    scaled = (w * np.exp2(127.0 - byte)[:, None, :]).reshape(k, n).astype(np.float32)
    c = np.ascontiguousarray(scaled.reshape(k // 512, 128, 4, n).transpose(0, 1, 3, 2)).astype(ml_dtypes.float4_e2m1fn).view(np.uint8) & 0xF
    words = (c[..., 0::2] | (c[..., 1::2] << 4)).reshape(k // 512, 128, 2 * n)
    return np.ascontiguousarray(words), np.ascontiguousarray(byte.astype(np.uint8).reshape(k // 512, 16, n))


def unpack_fp4(words, scales):
    g, _, n = scales.shape
    words = np.ascontiguousarray(words).reshape(g, 128, n, 2)
    nib = np.empty((g, 128, n, 4), np.uint8)
    nib[..., 0::2] = words & 0xF
    nib[..., 1::2] = words >> 4
    vals = E2M1[nib] * np.repeat(np.exp2(scales.astype(np.float64) - 127.0), 8, axis=1)[..., None]
    return vals.transpose(0, 1, 3, 2).reshape(g * 512, n)


def gelu(v):
    return 0.5 * v * (1.0 + np.tanh(np.sqrt(2.0 / np.pi) * (v + 0.044715 * v**3)))


K, T, S, N = 512, 2048, 1024, 128
P = 2 ** 7


def setup_inputs():
    n = np.random.standard_normal
    s = mx_kscale(K)[:, None]
    packed_w1 = pack_fp4(n((K, N)) / np.sqrt(K) / s)
    return {
        "xT": (n((K, T)) * s).astype(np.float32),
        "zp": np.tile(np.random.uniform(-0.6, 0.6, T), (P, 1)).astype(np.float32),
        "csum": n((N, 1)).astype(np.float32),
        "w1_words": packed_w1[0],
        "w1_scales": packed_w1[1],
        "offs": striped(np.random.permutation(T)[:S]),
    }


def reference(xT, zp, csum, w1_words, w1_scales, offs):
    xq = mxq(f64(xT)[:, unstriped(offs)], 0, "e4m3")
    y = unpack_fp4(w1_words, w1_scales).T @ xq
    zg = f64(zp)[:1][:, unstriped(offs)]
    return gelu(y - (f64(csum) * zg))

@@ -1,0 +1,147 @@
+from contextlib import ExitStack
+
+import concourse.mybir as mybir
+from concourse.masks import make_identity
+
+K, T, S, N = 512, 2048, 1024, 128
+P = 128
+FLOPS = 2 * K * S * N
+
+F32 = mybir.dt.float32
+BF16 = mybir.dt.bfloat16
+U32 = mybir.dt.uint32
+I32 = mybir.dt.int32
+U16 = mybir.dt.uint16
+U8 = mybir.dt.uint8
+FP8X4 = mybir.dt.float8_e4m3fn_x4
+FP4X4 = mybir.dt.float4_e2m1fn_x4
+ACT = mybir.ActivationFunctionType
+ALU = mybir.AluOpType
+
+CHUNK = 256
+CHUNKS = S // CHUNK
+LOADS = [(0, 0, 1024, 1024), (0, 1024, 1024, 384), (1, 0, 1024, 1024), (1, 1024, 512, 0), (1, 1536, 512, 192)]
+
+
+def tile_picked_zeropt_gelu_l_kernel(tc, xT, zp, csum, w1_words, w1_scales, offs, out):
+    nc = tc.nc
+    with ExitStack() as ctx:
+        keep = ctx.enter_context(tc.tile_pool(name="keep", bufs=1))
+        psum = ctx.enter_context(tc.psum_pool(name="psum", bufs=1))
+
+        offsets = keep.tile([P, S // 16], U16, name="offsets")
+
+        zp_table = keep.tile([P, T], F32, name="zp_table")
+        nc.vector.memset(zp_table[:, : T // 2], 0.0)
+        nc.gpsimd.memset(zp_table[:, T // 2 :], 0.0)
+        warm = keep.tile([P, 8], F32, name="warm")
+        nc.scalar.activation(warm[32:64, 0:1], zp_table[32:64, 0:1], ACT.Gelu_apprx_tanh)
+
+        rows = xT.rearrange("(p j) t -> p j t", j=4)
+        raws = []
+        for i, (pair, c0, width, on_scalar) in enumerate(LOADS):
+            raw = keep.tile([P, 2, width], F32, name=f"raw{i}")
+            nc.sync.dma_start(raw[:], rows[:, 2 * pair : 2 * pair + 2, c0 : c0 + width])
+            raws.append(raw)
+            if i == 0:
+                nc.sync.dma_start(offsets[:], offs)
+                nc.sync.dma_start(zp_table[0:1, :], zp[0:1, :])
+
+        w_words = keep.tile([P, 2 * N], U8, name="w_words", align_bytes=64)
+        w_scales = keep.tile([P, N], U8, name="w_scales", align_bytes=64)
+        csum_col = keep.tile([P, 1], F32, name="csum_col")
+        nc.sync.dma_start(csum_col[:], csum)
+        nc.sync.dma_start(w_words[:].bitcast(I32), w1_words[0].bitcast(I32))
+        nc.vector.memset(w_scales[:].bitcast(I32), 0)
+        for q in range(4):
+            nc.sync.dma_start(
+                w_scales[32 * q : 32 * q + 4, :].bitcast(I32),
+                w1_scales[0, 4 * q : 4 * q + 4, :].bitcast(I32),
+            )
+
+        identity = keep.tile([P, P], F32, name="identity")
+        make_identity(nc, identity[:])
+
+        zp_picked = keep.tile([P, S], F32, name="zp_picked")
+        nc.vector.tensor_copy(zp_picked[:], zp_table[:].indirect(offsets[:]))
+        zp_cols = keep.tile([P, S // P], F32, name="zp_cols")
+        for b in range(2):
+            turned = psum.tile([P, 4, P], F32, name=f"turned{b}")
+            for c in range(4):
+                j0 = (4 * b + c) * P
+                nc.tensor.transpose(turned[:, c, :], zp_picked[:, j0 : j0 + P], identity[:])
+            nc.scalar.copy(zp_cols[:, 4 * b : 4 * b + 4], turned[:, :, 0])
+        corrections = []
+        for b in range(2):
+            spread = psum.tile([P, 4, P], F32, name=f"spread{b}")
+            for c in range(4):
+                col = 4 * b + c
+                nc.tensor.transpose(spread[:, c, :], zp_cols[:, col : col + 1].to_broadcast([P, P]), identity[:])
+            correction = keep.tile([P, 4 * P], F32, name=f"correction{b}")
+            nc.scalar.activation(correction[:], spread[:].rearrange("p c j -> p (c j)"), ACT.Copy, scale=csum_col[:])
+            corrections.append(correction)
+
+        windows = [keep.tile([P, T, 2], BF16, name=f"window{u}") for u in range(2)]
+        grouped = [keep.tile([P, CHUNK, 4], BF16, name=f"grouped{c}", align_bytes=64) for c in range(CHUNKS)]
+
+        picked = [keep.tile([P, 2, CHUNK], U32, name=f"picked{c}") for c in range(CHUNKS)]
+
+        def cast(i):
+            pair, c0, width, on_scalar = LOADS[i]
+            src = raws[i][:].rearrange("p j t -> p t j")
+            if on_scalar > 0:
+                nc.scalar.copy(windows[pair][:, c0 : c0 + on_scalar, :], src[:, :on_scalar, :])
+            if on_scalar < width:
+                nc.vector.tensor_copy(windows[pair][:, c0 + on_scalar : c0 + width, :], src[:, on_scalar:, :])
+
+        def gather(pair, c):
+            words = windows[pair][:].rearrange("p t j -> p (t j)").bitcast(U32)
+            cols = CHUNK // 16
+            nc.vector.tensor_copy(picked[c][:, pair, :], words.indirect(offsets[:, c * cols : (c + 1) * cols]))
+
+        def weave(c):
+            dst = grouped[c][:].rearrange("p s j -> p (s j)").bitcast(U32).rearrange("p (s u) -> p s u", u=2)
+            nc.scalar.copy(dst, picked[c][:].rearrange("p u s -> p s u"))
+
+        sums = []
+
+        def multiply(c):
+            codes = keep.tile([P, CHUNK], U32, name=f"codes{c}", align_bytes=64)
+            scales = keep.tile([P, CHUNK], U8, name=f"scales{c}", align_bytes=64)
+            nc.vector.quantize_mx(
+                out=codes[:].bitcast(FP8X4), scales=scales[:], in_=grouped[c][:].rearrange("p s j -> p (s j)")
+            )
+            acc = psum.tile([P, CHUNK], F32, name=f"acc{c}")
+            nc.tensor.matmul_mx(
+                out=acc[:],
+                lhsT=w_words[:].bitcast(FP4X4),
+                lhsT_scale=w_scales[:],
+                rhs=codes[:].bitcast(FP8X4),
+                rhs_scale=scales[:],
+                start=True,
+                stop=True,
+            )
+            sums.append(acc)
+
+        def finish(c):
+            shifted = keep.tile([P, CHUNK], F32, name=f"shifted{c}")
+            half = corrections[c // 2][:, (c % 2) * CHUNK : (c % 2 + 1) * CHUNK]
+            nc.vector.tensor_tensor(shifted[:], sums[c][:], half, ALU.subtract)
+            result = keep.tile([P, CHUNK], F32, name=f"result{c}")
+            nc.scalar.activation(result[:], shifted[:], ACT.Gelu_apprx_tanh)
+            nc.sync.dma_start(out[:, c * CHUNK : (c + 1) * CHUNK], result[:])
+
+        cast(0)
+        cast(1)
+        for c in range(CHUNKS):
+            gather(0, c)
+        for i in range(2, len(LOADS)):
+            cast(i)
+        for c in range(CHUNKS):
+            gather(1, c)
+            weave(c)
+        for step in range(CHUNKS + 2):
+            if step < CHUNKS:
+                multiply(step)
+            if step >= 2:
+                finish(step - 2)

@@ -20,7 +20,7 @@ ALU = mybir.AluOpType
 
 CHUNK = 256
 CHUNKS = S // CHUNK
-LOADS = [(0, 0, 1024, 1024), (0, 1024, 1024, 384), (1, 0, 1024, 1024), (1, 1024, 512, 0), (1, 1536, 512, 192)]
+LOADS = [(0, 0, 1280, 0), (0, 1280, 768, 0), (1, 0, 1024, 768), (1, 1024, 768, 256), (1, 1792, 256, 80)]
 
 
 def tile_picked_zeropt_gelu_l_kernel(tc, xT, zp, csum, w1_words, w1_scales, offs, out):
@@ -32,20 +32,19 @@ def tile_picked_zeropt_gelu_l_kernel(tc, xT, zp, csum, w1_words, w1_scales, offs
         offsets = keep.tile([P, S // 16], U16, name="offsets")
 
         zp_table = keep.tile([P, T], F32, name="zp_table")
-        nc.vector.memset(zp_table[:, : T // 2], 0.0)
-        nc.gpsimd.memset(zp_table[:, T // 2 :], 0.0)
+        nc.sync.dma_start(zp_table[P - 1 : P, :], zp[0:1, :])
+        nc.sync.dma_start(offsets[:], offs)
+        nc.vector.memset(zp_table[: P - 1, : T // 2], 0.0)
+        nc.gpsimd.memset(zp_table[: P - 1, T // 2 :], 0.0)
         warm = keep.tile([P, 8], F32, name="warm")
         nc.scalar.activation(warm[32:64, 0:1], zp_table[32:64, 0:1], ACT.Gelu_apprx_tanh)
 
         rows = xT.rearrange("(p j) t -> p j t", j=4)
         raws = []
         for i, (pair, c0, width, on_scalar) in enumerate(LOADS):
-            raw = keep.tile([P, 2, width], F32, name=f"raw{i}")
+            raw = keep.tile([P, 2, width], F32, name=f"raw{i}", tag=f"raw{i}")
             nc.sync.dma_start(raw[:], rows[:, 2 * pair : 2 * pair + 2, c0 : c0 + width])
             raws.append(raw)
-            if i == 0:
-                nc.sync.dma_start(offsets[:], offs)
-                nc.sync.dma_start(zp_table[0:1, :], zp[0:1, :])
 
         w_words = keep.tile([P, 2 * N], U8, name="w_words", align_bytes=64)
         w_scales = keep.tile([P, N], U8, name="w_scales", align_bytes=64)
@@ -62,29 +61,35 @@ def tile_picked_zeropt_gelu_l_kernel(tc, xT, zp, csum, w1_words, w1_scales, offs
         identity = keep.tile([P, P], F32, name="identity")
         make_identity(nc, identity[:])
 
-        zp_picked = keep.tile([P, S], F32, name="zp_picked")
-        nc.vector.tensor_copy(zp_picked[:], zp_table[:].indirect(offsets[:]))
-        zp_cols = keep.tile([P, S // P], F32, name="zp_cols")
+        corrections = []
+        spreads = []
         for b in range(2):
+            zp_picked = keep.tile([P, 4 * P], F32, name=f"zp_picked{b}", tag=f"zp_picked{b}")
+            nc.vector.tensor_copy(zp_picked[:], zp_table[:].indirect(offsets[:, 32 * b : 32 * b + 32]))
             turned = psum.tile([P, 4, P], F32, name=f"turned{b}")
             for c in range(4):
-                j0 = (4 * b + c) * P
-                nc.tensor.transpose(turned[:, c, :], zp_picked[:, j0 : j0 + P], identity[:])
-            nc.scalar.copy(zp_cols[:, 4 * b : 4 * b + 4], turned[:, :, 0])
-        corrections = []
-        for b in range(2):
+                nc.tensor.transpose(turned[:, c, :], zp_picked[:, c * P : (c + 1) * P], identity[:])
+            cols = keep.tile([P, 4], F32, name=f"zp_cols{b}", tag=f"zp_cols{b}")
+            nc.scalar.copy(cols[:], turned[:, :, P - 1])
             spread = psum.tile([P, 4, P], F32, name=f"spread{b}")
             for c in range(4):
-                col = 4 * b + c
-                nc.tensor.transpose(spread[:, c, :], zp_cols[:, col : col + 1].to_broadcast([P, P]), identity[:])
-            correction = keep.tile([P, 4 * P], F32, name=f"correction{b}")
-            nc.scalar.activation(correction[:], spread[:].rearrange("p c j -> p (c j)"), ACT.Copy, scale=csum_col[:])
+                nc.tensor.transpose(spread[:, c, :], cols[:, c : c + 1].to_broadcast([P, P]), identity[:])
+            spreads.append(spread)
+
+        def correct(b, tag):
+            correction = keep.tile([P, 4 * P], F32, name=f"correction{b}", tag=tag)
+            nc.scalar.copy(correction[:], spreads[b][:].rearrange("p c j -> p (c j)"))
             corrections.append(correction)
 
-        windows = [keep.tile([P, T, 2], BF16, name=f"window{u}") for u in range(2)]
+        correct(0, "correction0")
+
+        windows = [
+            keep.tile([P, T, 2], BF16, name="window0"),
+            keep.tile([P, T, 2], BF16, name="window1", tag="zp_cols1"),
+        ]
         grouped = [keep.tile([P, CHUNK, 4], BF16, name=f"grouped{c}", align_bytes=64) for c in range(CHUNKS)]
 
-        picked = [keep.tile([P, 2, CHUNK], U32, name=f"picked{c}") for c in range(CHUNKS)]
+        picked = [keep.tile([P, 2, CHUNK], U32, name=f"picked{c}", tag=f"picked{c}") for c in range(CHUNKS)]
 
         def cast(i):
             pair, c0, width, on_scalar = LOADS[i]
@@ -123,13 +128,15 @@ def tile_picked_zeropt_gelu_l_kernel(tc, xT, zp, csum, w1_words, w1_scales, offs
             )
             sums.append(acc)
 
-        def finish(c):
-            shifted = keep.tile([P, CHUNK], F32, name=f"shifted{c}")
-            half = corrections[c // 2][:, (c % 2) * CHUNK : (c % 2 + 1) * CHUNK]
-            nc.vector.tensor_tensor(shifted[:], sums[c][:], half, ALU.subtract)
-            result = keep.tile([P, CHUNK], F32, name=f"result{c}")
-            nc.scalar.activation(result[:], shifted[:], ACT.Gelu_apprx_tanh)
-            nc.sync.dma_start(out[:, c * CHUNK : (c + 1) * CHUNK], result[:])
+        def finish(c, shifted, j0, width):
+            col = j0 - c * CHUNK
+            part = corrections[c // 2][:, j0 % (2 * CHUNK) : j0 % (2 * CHUNK) + width]
+            nc.vector.scalar_tensor_tensor(
+                shifted, part, csum_col[:], sums[c][:, col : col + width], ALU.mult, ALU.subtract
+            )
+            result = keep.tile([P, width], F32, name=f"result{j0}")
+            nc.scalar.activation(result[:], shifted, ACT.Gelu_apprx_tanh, scale=-1.0)
+            nc.sync.dma_start(out[:, j0 : j0 + width], result[:])
 
         cast(0)
         cast(1)
@@ -137,11 +144,16 @@ def tile_picked_zeropt_gelu_l_kernel(tc, xT, zp, csum, w1_words, w1_scales, offs
             gather(0, c)
         for i in range(2, len(LOADS)):
             cast(i)
+        correct(1, f"raw{len(LOADS) - 1}")
         for c in range(CHUNKS):
             gather(1, c)
             weave(c)
-        for step in range(CHUNKS + 2):
-            if step < CHUNKS:
-                multiply(step)
-            if step >= 2:
-                finish(step - 2)
+        for c in range(CHUNKS):
+            multiply(c)
+        early = keep.tile([P, 2, CHUNK], F32, name="early", tag=f"picked{CHUNKS - 1}")
+        late = keep.tile([P, 2, CHUNK], F32, name="late")
+        finish(0, early[:, 0, :], 0, CHUNK)
+        finish(1, early[:, 1, :], CHUNK, CHUNK)
+        finish(2, late[:, 0, :], 2 * CHUNK, CHUNK)
+        finish(3, late[:, 1, :128], 3 * CHUNK, 128)
+        finish(3, late[:, 1, 128:], 3 * CHUNK + 128, 128)

@@ -20,7 +20,7 @@ ALU = mybir.AluOpType
 
 CHUNK = 256
 CHUNKS = S // CHUNK
-LOADS = [(0, 0, 1280, 0), (0, 1280, 768, 0), (1, 0, 1024, 768), (1, 1024, 768, 256), (1, 1792, 256, 80)]
+LOADS = [(0, 0, 512, 512), (0, 512, 768, 768), (0, 1280, 768, 0), (1, 0, 1024, 768), (1, 1024, 768, 256), (1, 1792, 256, 80)]
 
 
 def tile_picked_zeropt_gelu_l_kernel(tc, xT, zp, csum, w1_words, w1_scales, offs, out):
@@ -32,8 +32,6 @@ def tile_picked_zeropt_gelu_l_kernel(tc, xT, zp, csum, w1_words, w1_scales, offs
         offsets = keep.tile([P, S // 16], U16, name="offsets")
 
         zp_table = keep.tile([P, T], F32, name="zp_table")
-        nc.sync.dma_start(zp_table[P - 1 : P, :], zp[0:1, :])
-        nc.sync.dma_start(offsets[:], offs)
         nc.vector.memset(zp_table[: P - 1, : T // 2], 0.0)
         nc.gpsimd.memset(zp_table[: P - 1, T // 2 :], 0.0)
         warm = keep.tile([P, 8], F32, name="warm")
@@ -45,6 +43,9 @@ def tile_picked_zeropt_gelu_l_kernel(tc, xT, zp, csum, w1_words, w1_scales, offs
             raw = keep.tile([P, 2, width], F32, name=f"raw{i}", tag=f"raw{i}")
             nc.sync.dma_start(raw[:], rows[:, 2 * pair : 2 * pair + 2, c0 : c0 + width])
             raws.append(raw)
+            if i == 0:
+                nc.sync.dma_start(zp_table[P - 1 : P, :], zp[0:1, :])
+                nc.sync.dma_start(offsets[:], offs)
 
         w_words = keep.tile([P, 2 * N], U8, name="w_words", align_bytes=64)
         w_scales = keep.tile([P, N], U8, name="w_scales", align_bytes=64)
@@ -85,7 +86,7 @@ def tile_picked_zeropt_gelu_l_kernel(tc, xT, zp, csum, w1_words, w1_scales, offs
 
         windows = [
             keep.tile([P, T, 2], BF16, name="window0"),
-            keep.tile([P, T, 2], BF16, name="window1", tag="zp_cols1"),
+            keep.tile([P, T, 2], BF16, name="window1", tag="zp_cols0"),
         ]
         grouped = [keep.tile([P, CHUNK, 4], BF16, name=f"grouped{c}", align_bytes=64) for c in range(CHUNKS)]
 
@@ -140,9 +141,10 @@ def tile_picked_zeropt_gelu_l_kernel(tc, xT, zp, csum, w1_words, w1_scales, offs
 
         cast(0)
         cast(1)
+        cast(2)
         for c in range(CHUNKS):
             gather(0, c)
-        for i in range(2, len(LOADS)):
+        for i in range(3, len(LOADS)):
             cast(i)
         correct(1, f"raw{len(LOADS) - 1}")
         for c in range(CHUNKS):
@@ -150,10 +152,7 @@ def tile_picked_zeropt_gelu_l_kernel(tc, xT, zp, csum, w1_words, w1_scales, offs
             weave(c)
         for c in range(CHUNKS):
             multiply(c)
-        early = keep.tile([P, 2, CHUNK], F32, name="early", tag=f"picked{CHUNKS - 1}")
-        late = keep.tile([P, 2, CHUNK], F32, name="late")
-        finish(0, early[:, 0, :], 0, CHUNK)
-        finish(1, early[:, 1, :], CHUNK, CHUNK)
-        finish(2, late[:, 0, :], 2 * CHUNK, CHUNK)
-        finish(3, late[:, 1, :128], 3 * CHUNK, 128)
-        finish(3, late[:, 1, 128:], 3 * CHUNK + 128, 128)
+        for c in range(CHUNKS):
+            tag = f"picked{c + 2}" if c < 2 else f"shifted{c}"
+            shifted = keep.tile([P, CHUNK], F32, name=f"shifted{c}", tag=tag)
+            finish(c, shifted[:], c * CHUNK, CHUNK)

@@ -20,7 +20,8 @@ ALU = mybir.AluOpType
 
 CHUNK = 256
 CHUNKS = S // CHUNK
-LOADS = [(0, 0, 512, 512), (0, 512, 768, 768), (0, 1280, 768, 0), (1, 0, 1024, 768), (1, 1024, 768, 256), (1, 1792, 256, 80)]
+PAIR_LOADS = [(0, 512, 512), (512, 512, 384), (1024, 448, 0), (1472, 320, 0), (1792, 256, 0)]
+LAST_LOADS = [(0, 256), (256, 512), (768, 512), (1280, 512), (1792, 256)]
 
 
 def tile_picked_zeropt_gelu_l_kernel(tc, xT, zp, csum, w1_words, w1_scales, offs, out):
@@ -38,14 +39,18 @@ def tile_picked_zeropt_gelu_l_kernel(tc, xT, zp, csum, w1_words, w1_scales, offs
         nc.scalar.activation(warm[32:64, 0:1], zp_table[32:64, 0:1], ACT.Gelu_apprx_tanh)
 
         rows = xT.rearrange("(p j) t -> p j t", j=4)
+        plane2 = keep.tile([P, T], F32, name="plane2", tag="plane2")
+        nc.sync.dma_start(zp_table[P - 1 : P, :], zp[0:1, :])
+        nc.sync.dma_start(offsets[:], offs)
+        nc.sync.dma_start(plane2[:], rows[:, 2, :])
         raws = []
-        for i, (pair, c0, width, on_scalar) in enumerate(LOADS):
+        for i, (c0, width, on_scalar) in enumerate(PAIR_LOADS):
             raw = keep.tile([P, 2, width], F32, name=f"raw{i}", tag=f"raw{i}")
-            nc.sync.dma_start(raw[:], rows[:, 2 * pair : 2 * pair + 2, c0 : c0 + width])
+            nc.sync.dma_start(raw[:], rows[:, 0:2, c0 : c0 + width])
             raws.append(raw)
-            if i == 0:
-                nc.sync.dma_start(zp_table[P - 1 : P, :], zp[0:1, :])
-                nc.sync.dma_start(offsets[:], offs)
+        plane3 = keep.tile([P, T], F32, name="plane3")
+        for c0, width in LAST_LOADS:
+            nc.sync.dma_start(plane3[:, c0 : c0 + width], rows[:, 3, c0 : c0 + width])
 
         w_words = keep.tile([P, 2 * N], U8, name="w_words", align_bytes=64)
         w_scales = keep.tile([P, N], U8, name="w_scales", align_bytes=64)
@@ -64,52 +69,64 @@ def tile_picked_zeropt_gelu_l_kernel(tc, xT, zp, csum, w1_words, w1_scales, offs
 
         corrections = []
         spreads = []
+        turneds = []
         for b in range(2):
             zp_picked = keep.tile([P, 4 * P], F32, name=f"zp_picked{b}", tag=f"zp_picked{b}")
             nc.vector.tensor_copy(zp_picked[:], zp_table[:].indirect(offsets[:, 32 * b : 32 * b + 32]))
             turned = psum.tile([P, 4, P], F32, name=f"turned{b}")
             for c in range(4):
                 nc.tensor.transpose(turned[:, c, :], zp_picked[:, c * P : (c + 1) * P], identity[:])
-            cols = keep.tile([P, 4], F32, name=f"zp_cols{b}", tag=f"zp_cols{b}")
-            nc.scalar.copy(cols[:], turned[:, :, P - 1])
+            turneds.append(turned)
+
+        def spread_out(b, tag):
+            cols = keep.tile([P, 4], F32, name=f"zp_cols{b}", tag=tag)
+            nc.scalar.copy(cols[:], turneds[b][:, :, P - 1])
             spread = psum.tile([P, 4, P], F32, name=f"spread{b}")
             for c in range(4):
                 nc.tensor.transpose(spread[:, c, :], cols[:, c : c + 1].to_broadcast([P, P]), identity[:])
             spreads.append(spread)
+
+        spread_out(0, "zp_cols0")
+        spread_out(1, "zp_cols1")
 
         def correct(b, tag):
             correction = keep.tile([P, 4 * P], F32, name=f"correction{b}", tag=tag)
             nc.scalar.copy(correction[:], spreads[b][:].rearrange("p c j -> p (c j)"))
             corrections.append(correction)
 
-        correct(0, "correction0")
+        pairs = keep.tile([P, T, 2], BF16, name="pairs", tag="zp_picked1")
+        rounded3 = keep.tile([P, T], BF16, name="rounded3", tag="zp_cols1")
+        grouped = [keep.tile([P, CHUNK, 4], BF16, name=f"grouped{c}", tag=f"grouped{c}", align_bytes=64) for c in range(CHUNKS)]
 
-        windows = [
-            keep.tile([P, T, 2], BF16, name="window0"),
-            keep.tile([P, T, 2], BF16, name="window1", tag="zp_cols0"),
-        ]
-        grouped = [keep.tile([P, CHUNK, 4], BF16, name=f"grouped{c}", align_bytes=64) for c in range(CHUNKS)]
+        def entries(c):
+            cols = CHUNK // 16
+            return offsets[:, c * cols : (c + 1) * cols]
 
-        picked = [keep.tile([P, 2, CHUNK], U32, name=f"picked{c}", tag=f"picked{c}") for c in range(CHUNKS)]
+        for c in range(CHUNKS):
+            nc.vector.tensor_copy(grouped[c][:, :, 2], plane2[:].indirect(entries(c)))
 
-        def cast(i):
-            pair, c0, width, on_scalar = LOADS[i]
+        for i, (c0, width, on_scalar) in enumerate(PAIR_LOADS):
             src = raws[i][:].rearrange("p j t -> p t j")
             if on_scalar > 0:
-                nc.scalar.copy(windows[pair][:, c0 : c0 + on_scalar, :], src[:, :on_scalar, :])
+                nc.scalar.copy(pairs[:, c0 : c0 + on_scalar, :], src[:, :on_scalar, :])
             if on_scalar < width:
-                nc.vector.tensor_copy(windows[pair][:, c0 + on_scalar : c0 + width, :], src[:, on_scalar:, :])
+                nc.vector.tensor_copy(pairs[:, c0 + on_scalar : c0 + width, :], src[:, on_scalar:, :])
+            if i == 1:
+                correct(0, "correction0")
+                correct(1, "plane2")
 
-        def gather(pair, c):
-            words = windows[pair][:].rearrange("p t j -> p (t j)").bitcast(U32)
-            cols = CHUNK // 16
-            nc.vector.tensor_copy(picked[c][:, pair, :], words.indirect(offsets[:, c * cols : (c + 1) * cols]))
-
-        def weave(c):
+        words = pairs[:].rearrange("p t j -> p (t j)").bitcast(U32)
+        for c in (1, 2, 3, 0):
             dst = grouped[c][:].rearrange("p s j -> p (s j)").bitcast(U32).rearrange("p (s u) -> p s u", u=2)
-            nc.scalar.copy(dst, picked[c][:].rearrange("p u s -> p s u"))
+            nc.vector.tensor_copy(dst[:, :, 0], words.indirect(entries(c)))
 
-        sums = []
+        for c0, width in LAST_LOADS:
+            nc.scalar.copy(rounded3[:, c0 : c0 + width], plane3[:, c0 : c0 + width])
+        for c in range(1, CHUNKS):
+            nc.scalar.activation(grouped[c][:, :, 3], rounded3[:].indirect(entries(c)), ACT.Copy)
+        nc.vector.tensor_copy(grouped[0][:, :, 3], plane3[:].indirect(entries(0)))
+
+        sums = {}
 
         def multiply(c):
             codes = keep.tile([P, CHUNK], U32, name=f"codes{c}", align_bytes=64)
@@ -127,32 +144,22 @@ def tile_picked_zeropt_gelu_l_kernel(tc, xT, zp, csum, w1_words, w1_scales, offs
                 start=True,
                 stop=True,
             )
-            sums.append(acc)
+            sums[c] = acc
 
-        def finish(c, shifted, j0, width):
-            col = j0 - c * CHUNK
-            part = corrections[c // 2][:, j0 % (2 * CHUNK) : j0 % (2 * CHUNK) + width]
-            nc.vector.scalar_tensor_tensor(
-                shifted, part, csum_col[:], sums[c][:, col : col + width], ALU.mult, ALU.subtract
-            )
-            result = keep.tile([P, width], F32, name=f"result{j0}")
-            nc.scalar.activation(result[:], shifted, ACT.Gelu_apprx_tanh, scale=-1.0)
-            nc.sync.dma_start(out[:, j0 : j0 + width], result[:])
+        def finish(c):
+            j0 = c * CHUNK
+            shifted = keep.tile([P, CHUNK], F32, name=f"shifted{c}")
+            part = corrections[c // 2][:, j0 % (2 * CHUNK) : j0 % (2 * CHUNK) + CHUNK]
+            nc.vector.scalar_tensor_tensor(shifted[:], part, csum_col[:], sums[c][:], ALU.mult, ALU.subtract)
+            result = keep.tile([P, CHUNK], F32, name=f"result{c}")
+            nc.scalar.activation(result[:], shifted[:], ACT.Gelu_apprx_tanh, scale=-1.0)
+            nc.sync.dma_start(out[:, j0 : j0 + CHUNK], result[:])
 
-        cast(0)
-        cast(1)
-        cast(2)
-        for c in range(CHUNKS):
-            gather(0, c)
-        for i in range(3, len(LOADS)):
-            cast(i)
-        correct(1, f"raw{len(LOADS) - 1}")
-        for c in range(CHUNKS):
-            gather(1, c)
-            weave(c)
-        for c in range(CHUNKS):
-            multiply(c)
-        for c in range(CHUNKS):
-            tag = f"picked{c + 2}" if c < 2 else f"shifted{c}"
-            shifted = keep.tile([P, CHUNK], F32, name=f"shifted{c}", tag=tag)
-            finish(c, shifted[:], c * CHUNK, CHUNK)
+        multiply(1)
+        multiply(0)
+        multiply(2)
+        finish(1)
+        multiply(3)
+        finish(0)
+        finish(2)
+        finish(3)

@@ -20,7 +20,7 @@ ALU = mybir.AluOpType
 
 CHUNK = 256
 CHUNKS = S // CHUNK
-PAIR_LOADS = [(0, 512, 512), (512, 512, 384), (1024, 448, 0), (1472, 320, 0), (1792, 256, 0)]
+PAIR_LOADS = [(0, 256, 256), (256, 512, 512), (768, 512, 512), (1280, 512, 0), (1792, 256, 0)]
 LAST_LOADS = [(0, 256), (256, 512), (768, 512), (1280, 512), (1792, 256)]
 
 
@@ -42,12 +42,13 @@ def tile_picked_zeropt_gelu_l_kernel(tc, xT, zp, csum, w1_words, w1_scales, offs
         plane2 = keep.tile([P, T], F32, name="plane2", tag="plane2")
         nc.sync.dma_start(zp_table[P - 1 : P, :], zp[0:1, :])
         nc.sync.dma_start(offsets[:], offs)
-        nc.sync.dma_start(plane2[:], rows[:, 2, :])
         raws = []
         for i, (c0, width, on_scalar) in enumerate(PAIR_LOADS):
             raw = keep.tile([P, 2, width], F32, name=f"raw{i}", tag=f"raw{i}")
             nc.sync.dma_start(raw[:], rows[:, 0:2, c0 : c0 + width])
             raws.append(raw)
+            if i == 0:
+                nc.sync.dma_start(plane2[:], rows[:, 2, :])
         plane3 = keep.tile([P, T], F32, name="plane3")
         for c0, width in LAST_LOADS:
             nc.sync.dma_start(plane3[:, c0 : c0 + width], rows[:, 3, c0 : c0 + width])
@@ -80,7 +81,10 @@ def tile_picked_zeropt_gelu_l_kernel(tc, xT, zp, csum, w1_words, w1_scales, offs
 
         def spread_out(b, tag):
             cols = keep.tile([P, 4], F32, name=f"zp_cols{b}", tag=tag)
-            nc.scalar.copy(cols[:], turneds[b][:, :, P - 1])
+            if b == 0:
+                nc.vector.tensor_copy(cols[:], turneds[b][:, :, P - 1])
+            else:
+                nc.scalar.copy(cols[:], turneds[b][:, :, P - 1])
             spread = psum.tile([P, 4, P], F32, name=f"spread{b}")
             for c in range(4):
                 nc.tensor.transpose(spread[:, c, :], cols[:, c : c + 1].to_broadcast([P, P]), identity[:])
@@ -94,8 +98,8 @@ def tile_picked_zeropt_gelu_l_kernel(tc, xT, zp, csum, w1_words, w1_scales, offs
             nc.scalar.copy(correction[:], spreads[b][:].rearrange("p c j -> p (c j)"))
             corrections.append(correction)
 
-        pairs = keep.tile([P, T, 2], BF16, name="pairs", tag="zp_picked1")
-        rounded3 = keep.tile([P, T], BF16, name="rounded3", tag="zp_cols1")
+        pairs = keep.tile([P, T, 2], BF16, name="pairs")
+        rounded3 = keep.tile([P, T], BF16, name="rounded3", tag="plane2")
         grouped = [keep.tile([P, CHUNK, 4], BF16, name=f"grouped{c}", tag=f"grouped{c}", align_bytes=64) for c in range(CHUNKS)]
 
         def entries(c):
@@ -113,7 +117,6 @@ def tile_picked_zeropt_gelu_l_kernel(tc, xT, zp, csum, w1_words, w1_scales, offs
                 nc.vector.tensor_copy(pairs[:, c0 + on_scalar : c0 + width, :], src[:, on_scalar:, :])
             if i == 1:
                 correct(0, "correction0")
-                correct(1, "plane2")
 
         words = pairs[:].rearrange("p t j -> p (t j)").bitcast(U32)
         for c in (1, 2, 3, 0):
@@ -124,6 +127,7 @@ def tile_picked_zeropt_gelu_l_kernel(tc, xT, zp, csum, w1_words, w1_scales, offs
             nc.scalar.copy(rounded3[:, c0 : c0 + width], plane3[:, c0 : c0 + width])
         for c in range(1, CHUNKS):
             nc.scalar.activation(grouped[c][:, :, 3], rounded3[:].indirect(entries(c)), ACT.Copy)
+        correct(1, "plane2")
         nc.vector.tensor_copy(grouped[0][:, :, 3], plane3[:].indirect(entries(0)))
 
         sums = {}
@@ -155,11 +159,11 @@ def tile_picked_zeropt_gelu_l_kernel(tc, xT, zp, csum, w1_words, w1_scales, offs
             nc.scalar.activation(result[:], shifted[:], ACT.Gelu_apprx_tanh, scale=-1.0)
             nc.sync.dma_start(out[:, j0 : j0 + CHUNK], result[:])
 
-        multiply(1)
         multiply(0)
+        multiply(1)
         multiply(2)
-        finish(1)
         multiply(3)
         finish(0)
+        finish(1)
         finish(2)
         finish(3)

@@ -21,7 +21,7 @@ ALU = mybir.AluOpType
 CHUNK = 256
 CHUNKS = S // CHUNK
 PAIR_LOADS = [(0, 256, 256), (256, 512, 512), (768, 512, 512), (1280, 512, 0), (1792, 256, 0)]
-LAST_LOADS = [(0, 256), (256, 512), (768, 512), (1280, 512), (1792, 256)]
+LAST_LOADS = [(0, 256), (256, 384), (640, 384), (1024, 384), (1408, 384), (1792, 256)]
 
 
 def tile_picked_zeropt_gelu_l_kernel(tc, xT, zp, csum, w1_words, w1_scales, offs, out):
@@ -72,7 +72,7 @@ def tile_picked_zeropt_gelu_l_kernel(tc, xT, zp, csum, w1_words, w1_scales, offs
         spreads = []
         turneds = []
         for b in range(2):
-            zp_picked = keep.tile([P, 4 * P], F32, name=f"zp_picked{b}", tag=f"zp_picked{b}")
+            zp_picked = keep.tile([P, 4 * P], F32, name=f"zp_picked{b}", tag=f"zp_picked{b}", align_bytes=64)
             nc.vector.tensor_copy(zp_picked[:], zp_table[:].indirect(offsets[:, 32 * b : 32 * b + 32]))
             turned = psum.tile([P, 4, P], F32, name=f"turned{b}")
             for c in range(4):
@@ -100,13 +100,14 @@ def tile_picked_zeropt_gelu_l_kernel(tc, xT, zp, csum, w1_words, w1_scales, offs
 
         pairs = keep.tile([P, T, 2], BF16, name="pairs")
         rounded3 = keep.tile([P, T], BF16, name="rounded3", tag="plane2")
-        grouped = [keep.tile([P, CHUNK, 4], BF16, name=f"grouped{c}", tag=f"grouped{c}", align_bytes=64) for c in range(CHUNKS)]
+        slots = ["zp_picked0", "zp_picked1", "grouped2", "grouped3"]
+        grouped = [keep.tile([P, CHUNK, 4], BF16, name=f"grouped{c}", tag=slots[c], align_bytes=64) for c in range(CHUNKS)]
 
         def entries(c):
             cols = CHUNK // 16
             return offsets[:, c * cols : (c + 1) * cols]
 
-        for c in range(CHUNKS):
+        for c in (2, 3, 0, 1):
             nc.vector.tensor_copy(grouped[c][:, :, 2], plane2[:].indirect(entries(c)))
 
         for i, (c0, width, on_scalar) in enumerate(PAIR_LOADS):
@@ -119,21 +120,21 @@ def tile_picked_zeropt_gelu_l_kernel(tc, xT, zp, csum, w1_words, w1_scales, offs
                 correct(0, "correction0")
 
         words = pairs[:].rearrange("p t j -> p (t j)").bitcast(U32)
-        for c in (1, 2, 3, 0):
+        for c in (0, 1, 3, 2):
             dst = grouped[c][:].rearrange("p s j -> p (s j)").bitcast(U32).rearrange("p (s u) -> p s u", u=2)
             nc.vector.tensor_copy(dst[:, :, 0], words.indirect(entries(c)))
 
         for c0, width in LAST_LOADS:
             nc.scalar.copy(rounded3[:, c0 : c0 + width], plane3[:, c0 : c0 + width])
-        for c in range(1, CHUNKS):
+        for c in (0, 1, 3):
             nc.scalar.activation(grouped[c][:, :, 3], rounded3[:].indirect(entries(c)), ACT.Copy)
         correct(1, "plane2")
-        nc.vector.tensor_copy(grouped[0][:, :, 3], plane3[:].indirect(entries(0)))
+        nc.vector.tensor_copy(grouped[2][:, :, 3], plane3[:].indirect(entries(2)))
 
         sums = {}
 
         def multiply(c):
-            codes = keep.tile([P, CHUNK], U32, name=f"codes{c}", align_bytes=64)
+            codes = keep.tile([P, CHUNK], U32, name=f"codes{c}", tag="zp_picked0" if c == 2 else f"codes{c}", align_bytes=64)
             scales = keep.tile([P, CHUNK], U8, name=f"scales{c}", align_bytes=64)
             nc.vector.quantize_mx(
                 out=codes[:].bitcast(FP8X4), scales=scales[:], in_=grouped[c][:].rearrange("p s j -> p (s j)")

@@ -20,38 +20,36 @@ ALU = mybir.AluOpType
 
 CHUNK = 256
 CHUNKS = S // CHUNK
-PAIR_LOADS = [(0, 256, 256), (256, 512, 512), (768, 512, 512), (1280, 512, 0), (1792, 256, 0)]
-LAST_LOADS = [(0, 256), (256, 384), (640, 384), (1024, 384), (1408, 384), (1792, 256)]
+LAST_PIECES = 4
+PLANE2_AT = 0
 
 
 def tile_picked_zeropt_gelu_l_kernel(tc, xT, zp, csum, w1_words, w1_scales, offs, out):
     nc = tc.nc
     with ExitStack() as ctx:
         keep = ctx.enter_context(tc.tile_pool(name="keep", bufs=1))
+        staged = ctx.enter_context(tc.tile_pool(name="staged", bufs=1))
         psum = ctx.enter_context(tc.psum_pool(name="psum", bufs=1))
 
         offsets = keep.tile([P, S // 16], U16, name="offsets")
 
         zp_table = keep.tile([P, T], F32, name="zp_table")
-        nc.vector.memset(zp_table[: P - 1, : T // 2], 0.0)
-        nc.gpsimd.memset(zp_table[: P - 1, T // 2 :], 0.0)
+        nc.vector.memset(zp_table[: P - 1, :], 0.0)
         warm = keep.tile([P, 8], F32, name="warm")
         nc.scalar.activation(warm[32:64, 0:1], zp_table[32:64, 0:1], ACT.Gelu_apprx_tanh)
 
         rows = xT.rearrange("(p j) t -> p j t", j=4)
-        plane2 = keep.tile([P, T], F32, name="plane2", tag="plane2")
+        planes = [
+            staged.tile([P, T], F32, name="plane2", offset=PLANE2_AT) if t == 2 else keep.tile([P, T], F32, name=f"plane{t}")
+            for t in range(4)
+        ]
         nc.sync.dma_start(zp_table[P - 1 : P, :], zp[0:1, :])
         nc.sync.dma_start(offsets[:], offs)
-        raws = []
-        for i, (c0, width, on_scalar) in enumerate(PAIR_LOADS):
-            raw = keep.tile([P, 2, width], F32, name=f"raw{i}", tag=f"raw{i}")
-            nc.sync.dma_start(raw[:], rows[:, 0:2, c0 : c0 + width])
-            raws.append(raw)
-            if i == 0:
-                nc.sync.dma_start(plane2[:], rows[:, 2, :])
-        plane3 = keep.tile([P, T], F32, name="plane3")
-        for c0, width in LAST_LOADS:
-            nc.sync.dma_start(plane3[:, c0 : c0 + width], rows[:, 3, c0 : c0 + width])
+        for t in (2, 0, 1):
+            nc.sync.dma_start(planes[t][:], rows[:, t, :])
+        width = T // LAST_PIECES
+        for i in range(LAST_PIECES):
+            nc.sync.dma_start(planes[3][:, i * width : (i + 1) * width], rows[:, 3, i * width : (i + 1) * width])
 
         w_words = keep.tile([P, 2 * N], U8, name="w_words", align_bytes=64)
         w_scales = keep.tile([P, N], U8, name="w_scales", align_bytes=64)
@@ -68,73 +66,72 @@ def tile_picked_zeropt_gelu_l_kernel(tc, xT, zp, csum, w1_words, w1_scales, offs
         identity = keep.tile([P, P], F32, name="identity")
         make_identity(nc, identity[:])
 
-        corrections = []
-        spreads = []
+        def entries(c):
+            cols = CHUNK // 16
+            return offsets[:, c * cols : (c + 1) * cols]
+
+        zp_picked = keep.tile([P, 2, 4 * P], F32, name="zp_picked")
         turneds = []
         for b in range(2):
-            zp_picked = keep.tile([P, 4 * P], F32, name=f"zp_picked{b}", tag=f"zp_picked{b}", align_bytes=64)
-            nc.vector.tensor_copy(zp_picked[:], zp_table[:].indirect(offsets[:, 32 * b : 32 * b + 32]))
+            nc.vector.tensor_copy(zp_picked[:, b, :], zp_table[:].indirect(offsets[:, 32 * b : 32 * b + 32]))
             turned = psum.tile([P, 4, P], F32, name=f"turned{b}")
             for c in range(4):
-                nc.tensor.transpose(turned[:, c, :], zp_picked[:, c * P : (c + 1) * P], identity[:])
+                nc.tensor.transpose(turned[:, c, :], zp_picked[:, b, c * P : (c + 1) * P], identity[:])
             turneds.append(turned)
+        words = [keep.tile([P, 2, CHUNK, 2], BF16, name=f"words{c}") for c in range(CHUNKS)]
 
-        def spread_out(b, tag):
-            cols = keep.tile([P, 4], F32, name=f"zp_cols{b}", tag=tag)
-            if b == 0:
-                nc.vector.tensor_copy(cols[:], turneds[b][:, :, P - 1])
-            else:
-                nc.scalar.copy(cols[:], turneds[b][:, :, P - 1])
+        rounded2 = keep.tile([P, T], BF16, name="rounded2")
+        nc.scalar.copy(rounded2[:], planes[2][:])
+        for c in range(2):
+            nc.vector.tensor_copy(words[c][:, 1, :, 0], planes[2][:].indirect(entries(c)))
+        spreads = []
+        for b in range(2):
+            cols = staged.tile([P, 4], F32, name=f"zp_cols{b}", offset=PLANE2_AT + S * 4 + 32 * b)
+            nc.scalar.copy(cols[:], turneds[b][:, :, P - 1])
             spread = psum.tile([P, 4, P], F32, name=f"spread{b}")
             for c in range(4):
                 nc.tensor.transpose(spread[:, c, :], cols[:, c : c + 1].to_broadcast([P, P]), identity[:])
             spreads.append(spread)
 
-        spread_out(0, "zp_cols0")
-        spread_out(1, "zp_cols1")
+        for c in range(2, CHUNKS):
+            nc.scalar.activation(words[c][:, 1, :, 0], rounded2[:].indirect(entries(c)), ACT.Copy)
 
-        def correct(b, tag):
-            correction = keep.tile([P, 4 * P], F32, name=f"correction{b}", tag=tag)
-            nc.scalar.copy(correction[:], spreads[b][:].rearrange("p c j -> p (c j)"))
-            corrections.append(correction)
+        picked_zp = staged.tile([P, S], F32, name="picked_zp", offset=PLANE2_AT)
+        for b in range(2):
+            nc.scalar.copy(picked_zp[:, b * 4 * P : (b + 1) * 4 * P], spreads[b][:].rearrange("p c j -> p (c j)"))
 
-        pairs = keep.tile([P, T, 2], BF16, name="pairs")
-        rounded3 = keep.tile([P, T], BF16, name="rounded3", tag="plane2")
-        slots = ["zp_picked0", "zp_picked1", "grouped2", "grouped3"]
-        grouped = [keep.tile([P, CHUNK, 4], BF16, name=f"grouped{c}", tag=slots[c], align_bytes=64) for c in range(CHUNKS)]
+        for t in range(2):
+            for c in range(CHUNKS):
+                nc.vector.tensor_copy(words[c][:, 0, :, t], planes[t][:].indirect(entries(c)))
 
-        def entries(c):
-            cols = CHUNK // 16
-            return offsets[:, c * cols : (c + 1) * cols]
+        rounded3 = staged.tile([P, T], BF16, name="rounded3", offset=PLANE2_AT + S * 4)
+        for i in range(LAST_PIECES):
+            nc.scalar.copy(rounded3[:, i * width : (i + 1) * width], planes[3][:, i * width : (i + 1) * width])
+        nc.vector.tensor_copy(words[0][:, 1, :, 1], planes[3][:].indirect(entries(0)))
+        for c in range(1, CHUNKS):
+            nc.scalar.activation(words[c][:, 1, :, 1], rounded3[:].indirect(entries(c)), ACT.Copy)
 
-        for c in (2, 3, 0, 1):
-            nc.vector.tensor_copy(grouped[c][:, :, 2], plane2[:].indirect(entries(c)))
-
-        for i, (c0, width, on_scalar) in enumerate(PAIR_LOADS):
-            src = raws[i][:].rearrange("p j t -> p t j")
-            if on_scalar > 0:
-                nc.scalar.copy(pairs[:, c0 : c0 + on_scalar, :], src[:, :on_scalar, :])
-            if on_scalar < width:
-                nc.vector.tensor_copy(pairs[:, c0 + on_scalar : c0 + width, :], src[:, on_scalar:, :])
-            if i == 1:
-                correct(0, "correction0")
-
-        words = pairs[:].rearrange("p t j -> p (t j)").bitcast(U32)
-        for c in (0, 1, 3, 2):
-            dst = grouped[c][:].rearrange("p s j -> p (s j)").bitcast(U32).rearrange("p (s u) -> p s u", u=2)
-            nc.vector.tensor_copy(dst[:, :, 0], words.indirect(entries(c)))
-
-        for c0, width in LAST_LOADS:
-            nc.scalar.copy(rounded3[:, c0 : c0 + width], plane3[:, c0 : c0 + width])
-        for c in (0, 1, 3):
-            nc.scalar.activation(grouped[c][:, :, 3], rounded3[:].indirect(entries(c)), ACT.Copy)
-        correct(1, "plane2")
-        nc.vector.tensor_copy(grouped[2][:, :, 3], plane3[:].indirect(entries(2)))
-
+        grouped = {}
         sums = {}
 
+        def join(c):
+            tile = keep.tile([P, CHUNK, 4], BF16, name=f"grouped{c}", tag=f"grouped{c}", align_bytes=64)
+            flat_in = words[c][:].rearrange("p u s e -> p (u s e)")
+            flat_out = tile[:].rearrange("p s j -> p (s j)")
+            if c < CHUNKS - 1:
+                nc.vector.tensor_copy(
+                    flat_out.bitcast(I32).rearrange("p (s u) -> p s u", u=2),
+                    flat_in.bitcast(I32).rearrange("p (u s) -> p s u", u=2),
+                )
+            else:
+                nc.scalar.copy(
+                    flat_out.bitcast(U32).rearrange("p (s u) -> p s u", u=2),
+                    flat_in.bitcast(U32).rearrange("p (u s) -> p s u", u=2),
+                )
+            grouped[c] = tile
+
         def multiply(c):
-            codes = keep.tile([P, CHUNK], U32, name=f"codes{c}", tag="zp_picked0" if c == 2 else f"codes{c}", align_bytes=64)
+            codes = keep.tile([P, CHUNK], U32, name=f"codes{c}", align_bytes=64)
             scales = keep.tile([P, CHUNK], U8, name=f"scales{c}", align_bytes=64)
             nc.vector.quantize_mx(
                 out=codes[:].bitcast(FP8X4), scales=scales[:], in_=grouped[c][:].rearrange("p s j -> p (s j)")
@@ -153,18 +150,23 @@ def tile_picked_zeropt_gelu_l_kernel(tc, xT, zp, csum, w1_words, w1_scales, offs
 
         def finish(c):
             j0 = c * CHUNK
-            shifted = keep.tile([P, CHUNK], F32, name=f"shifted{c}")
-            part = corrections[c // 2][:, j0 % (2 * CHUNK) : j0 % (2 * CHUNK) + CHUNK]
-            nc.vector.scalar_tensor_tensor(shifted[:], part, csum_col[:], sums[c][:], ALU.mult, ALU.subtract)
+            tag = f"grouped{CHUNKS - 1}" if c == 1 else f"shifted{c}"
+            shifted = keep.tile([P, CHUNK], F32, name=f"shifted{c}", tag=tag, align_bytes=64)
+            nc.vector.scalar_tensor_tensor(
+                shifted[:], picked_zp[:, j0 : j0 + CHUNK], csum_col[:], sums[c][:], ALU.mult, ALU.subtract
+            )
             result = keep.tile([P, CHUNK], F32, name=f"result{c}")
             nc.scalar.activation(result[:], shifted[:], ACT.Gelu_apprx_tanh, scale=-1.0)
             nc.sync.dma_start(out[:, j0 : j0 + CHUNK], result[:])
 
+        join(0)
+        join(1)
         multiply(0)
+        join(2)
+        join(3)
         multiply(1)
         multiply(2)
-        multiply(3)
         finish(0)
-        finish(1)
-        finish(2)
-        finish(3)
+        multiply(3)
+        for c in range(1, CHUNKS):
+            finish(c)

@@ -20,8 +20,12 @@ ALU = mybir.AluOpType
 
 CHUNK = 256
 CHUNKS = S // CHUNK
-LAST_PIECES = 4
+LAST_PIECES = [(0, 608), (608, 1152), (1152, 1632), (1632, 2048)]
 PLANE2_AT = 0
+WORDS_AT = PLANE2_AT + T * 4
+ROUNDED_AT = WORDS_AT + S * 8
+RUN = 4
+CAST_SPLIT = 1536
 
 
 def tile_picked_zeropt_gelu_l_kernel(tc, xT, zp, csum, w1_words, w1_scales, offs, out):
@@ -34,7 +38,9 @@ def tile_picked_zeropt_gelu_l_kernel(tc, xT, zp, csum, w1_words, w1_scales, offs
         offsets = keep.tile([P, S // 16], U16, name="offsets")
 
         zp_table = keep.tile([P, T], F32, name="zp_table")
-        nc.vector.memset(zp_table[: P - 1, :], 0.0)
+        nc.vector.memset(zp_table[: P - 1, :1280], 0.0)
+        nc.gpsimd.memset(zp_table[: P - 1, 1280:], 0.0)
+        nc.scalar.dma_start(zp_table[P - 1 : P, :], zp[0:1, :])
         warm = keep.tile([P, 8], F32, name="warm")
         nc.scalar.activation(warm[32:64, 0:1], zp_table[32:64, 0:1], ACT.Gelu_apprx_tanh)
 
@@ -43,13 +49,11 @@ def tile_picked_zeropt_gelu_l_kernel(tc, xT, zp, csum, w1_words, w1_scales, offs
             staged.tile([P, T], F32, name="plane2", offset=PLANE2_AT) if t == 2 else keep.tile([P, T], F32, name=f"plane{t}")
             for t in range(4)
         ]
-        nc.sync.dma_start(zp_table[P - 1 : P, :], zp[0:1, :])
         nc.sync.dma_start(offsets[:], offs)
         for t in (2, 0, 1):
             nc.sync.dma_start(planes[t][:], rows[:, t, :])
-        width = T // LAST_PIECES
-        for i in range(LAST_PIECES):
-            nc.sync.dma_start(planes[3][:, i * width : (i + 1) * width], rows[:, 3, i * width : (i + 1) * width])
+        for lo, hi in LAST_PIECES:
+            nc.sync.dma_start(planes[3][:, lo:hi], rows[:, 3, lo:hi])
 
         w_words = keep.tile([P, 2 * N], U8, name="w_words", align_bytes=64)
         w_scales = keep.tile([P, N], U8, name="w_scales", align_bytes=64)
@@ -70,43 +74,44 @@ def tile_picked_zeropt_gelu_l_kernel(tc, xT, zp, csum, w1_words, w1_scales, offs
             cols = CHUNK // 16
             return offsets[:, c * cols : (c + 1) * cols]
 
-        zp_picked = keep.tile([P, 2, 4 * P], F32, name="zp_picked")
+        zp_picked = staged.tile([P, 2, 4 * P], F32, name="zp_picked", offset=WORDS_AT)
         turneds = []
         for b in range(2):
-            nc.vector.tensor_copy(zp_picked[:, b, :], zp_table[:].indirect(offsets[:, 32 * b : 32 * b + 32]))
+            for lo, hi in ((0, 512),) if b == 0 else ((0, 256), (256, 512)):
+                first = (512 * b + lo) // 16
+                nc.vector.tensor_copy(zp_picked[:, b, lo:hi], zp_table[:].indirect(offsets[:, first : first + (hi - lo) // 16]))
             turned = psum.tile([P, 4, P], F32, name=f"turned{b}")
             for c in range(4):
                 nc.tensor.transpose(turned[:, c, :], zp_picked[:, b, c * P : (c + 1) * P], identity[:])
             turneds.append(turned)
-        words = [keep.tile([P, 2, CHUNK, 2], BF16, name=f"words{c}") for c in range(CHUNKS)]
-
-        rounded2 = keep.tile([P, T], BF16, name="rounded2")
-        nc.scalar.copy(rounded2[:], planes[2][:])
-        for c in range(2):
-            nc.vector.tensor_copy(words[c][:, 1, :, 0], planes[2][:].indirect(entries(c)))
         spreads = []
         for b in range(2):
-            cols = staged.tile([P, 4], F32, name=f"zp_cols{b}", offset=PLANE2_AT + S * 4 + 32 * b)
-            nc.scalar.copy(cols[:], turneds[b][:, :, P - 1])
+            cols = staged.tile([P, 4], F32, name=f"zp_cols{b}", offset=ROUNDED_AT + T * 2 + 32 * b)
+            nc.vector.tensor_copy(cols[:], turneds[b][:, :, P - 1])
             spread = psum.tile([P, 4, P], F32, name=f"spread{b}")
             for c in range(4):
                 nc.tensor.transpose(spread[:, c, :], cols[:, c : c + 1].to_broadcast([P, P]), identity[:])
             spreads.append(spread)
 
-        for c in range(2, CHUNKS):
-            nc.scalar.activation(words[c][:, 1, :, 0], rounded2[:].indirect(entries(c)), ACT.Copy)
+        all_words = staged.tile([P, 2, S, 2], BF16, name="all_words", offset=WORDS_AT)
+        words = [all_words[:, :, c * CHUNK : (c + 1) * CHUNK, :] for c in range(CHUNKS)]
+
+        rounded2 = staged.tile([P, T], BF16, name="rounded2", offset=ROUNDED_AT)
+        nc.scalar.copy(rounded2[:, :CAST_SPLIT], planes[2][:, :CAST_SPLIT])
+        nc.vector.tensor_copy(rounded2[:, CAST_SPLIT:], planes[2][:, CAST_SPLIT:])
+        nc.vector.tensor_copy(words[0][:, 1, :, 0], planes[2][:].indirect(entries(0)))
+        nc.scalar.activation(all_words[:, 1, CHUNK:, 0], rounded2[:].indirect(offsets[:, CHUNK // 16 :]), ACT.Copy)
 
         picked_zp = staged.tile([P, S], F32, name="picked_zp", offset=PLANE2_AT)
         for b in range(2):
             nc.scalar.copy(picked_zp[:, b * 4 * P : (b + 1) * 4 * P], spreads[b][:].rearrange("p c j -> p (c j)"))
 
         for t in range(2):
-            for c in range(CHUNKS):
-                nc.vector.tensor_copy(words[c][:, 0, :, t], planes[t][:].indirect(entries(c)))
+            nc.vector.tensor_copy(all_words[:, 0, :, t], planes[t][:].indirect(offsets[:]))
 
-        rounded3 = staged.tile([P, T], BF16, name="rounded3", offset=PLANE2_AT + S * 4)
-        for i in range(LAST_PIECES):
-            nc.scalar.copy(rounded3[:, i * width : (i + 1) * width], planes[3][:, i * width : (i + 1) * width])
+        rounded3 = staged.tile([P, T], BF16, name="rounded3", offset=ROUNDED_AT + 64)
+        for lo, hi in LAST_PIECES:
+            nc.scalar.copy(rounded3[:, lo:hi], planes[3][:, lo:hi])
         nc.vector.tensor_copy(words[0][:, 1, :, 1], planes[3][:].indirect(entries(0)))
         for c in range(1, CHUNKS):
             nc.scalar.activation(words[c][:, 1, :, 1], rounded3[:].indirect(entries(c)), ACT.Copy)
@@ -116,18 +121,15 @@ def tile_picked_zeropt_gelu_l_kernel(tc, xT, zp, csum, w1_words, w1_scales, offs
 
         def join(c):
             tile = keep.tile([P, CHUNK, 4], BF16, name=f"grouped{c}", tag=f"grouped{c}", align_bytes=64)
-            flat_in = words[c][:].rearrange("p u s e -> p (u s e)")
-            flat_out = tile[:].rearrange("p s j -> p (s j)")
+            word = I32 if c < CHUNKS - 1 else U32
+            src = all_words[:].rearrange("p u s e -> p u (s e)").bitcast(word)[:, :, c * CHUNK : (c + 1) * CHUNK]
+            dst = tile[:].rearrange("p s j -> p (s j)").bitcast(word)
+            src = src.rearrange("p u (g i) -> p g u i", i=RUN)
+            dst = dst.rearrange("p (g i u) -> p g u i", i=RUN, u=2)
             if c < CHUNKS - 1:
-                nc.vector.tensor_copy(
-                    flat_out.bitcast(I32).rearrange("p (s u) -> p s u", u=2),
-                    flat_in.bitcast(I32).rearrange("p (u s) -> p s u", u=2),
-                )
+                nc.vector.tensor_copy(dst, src)
             else:
-                nc.scalar.copy(
-                    flat_out.bitcast(U32).rearrange("p (s u) -> p s u", u=2),
-                    flat_in.bitcast(U32).rearrange("p (u s) -> p s u", u=2),
-                )
+                nc.scalar.copy(dst, src)
             grouped[c] = tile
 
         def multiply(c):
@@ -157,7 +159,8 @@ def tile_picked_zeropt_gelu_l_kernel(tc, xT, zp, csum, w1_words, w1_scales, offs
             )
             result = keep.tile([P, CHUNK], F32, name=f"result{c}")
             nc.scalar.activation(result[:], shifted[:], ACT.Gelu_apprx_tanh, scale=-1.0)
-            nc.sync.dma_start(out[:, j0 : j0 + CHUNK], result[:])
+            queue = nc.scalar if c == CHUNKS - 1 else nc.sync
+            queue.dma_start(out[:, j0 : j0 + CHUNK], result[:])
 
         join(0)
         join(1)

@@ -20,12 +20,9 @@ ALU = mybir.AluOpType
 
 CHUNK = 256
 CHUNKS = S // CHUNK
-LAST_PIECES = [(0, 608), (608, 1152), (1152, 1632), (1632, 2048)]
+LAST_PIECES = [(0, 512), (512, 1024), (1024, 1536), (1536, 2048)]
+LOW_AT = 1536
 PLANE2_AT = 0
-WORDS_AT = PLANE2_AT + T * 4
-ROUNDED_AT = WORDS_AT + S * 8
-RUN = 4
-CAST_SPLIT = 1536
 
 
 def tile_picked_zeropt_gelu_l_kernel(tc, xT, zp, csum, w1_words, w1_scales, offs, out):
@@ -38,9 +35,7 @@ def tile_picked_zeropt_gelu_l_kernel(tc, xT, zp, csum, w1_words, w1_scales, offs
         offsets = keep.tile([P, S // 16], U16, name="offsets")
 
         zp_table = keep.tile([P, T], F32, name="zp_table")
-        nc.vector.memset(zp_table[: P - 1, :1280], 0.0)
-        nc.gpsimd.memset(zp_table[: P - 1, 1280:], 0.0)
-        nc.scalar.dma_start(zp_table[P - 1 : P, :], zp[0:1, :])
+        nc.vector.memset(zp_table[: P - 1, :], 0.0)
         warm = keep.tile([P, 8], F32, name="warm")
         nc.scalar.activation(warm[32:64, 0:1], zp_table[32:64, 0:1], ACT.Gelu_apprx_tanh)
 
@@ -49,6 +44,7 @@ def tile_picked_zeropt_gelu_l_kernel(tc, xT, zp, csum, w1_words, w1_scales, offs
             staged.tile([P, T], F32, name="plane2", offset=PLANE2_AT) if t == 2 else keep.tile([P, T], F32, name=f"plane{t}")
             for t in range(4)
         ]
+        nc.sync.dma_start(zp_table[P - 1 : P, :], zp[0:1, :])
         nc.sync.dma_start(offsets[:], offs)
         for t in (2, 0, 1):
             nc.sync.dma_start(planes[t][:], rows[:, t, :])
@@ -74,63 +70,75 @@ def tile_picked_zeropt_gelu_l_kernel(tc, xT, zp, csum, w1_words, w1_scales, offs
             cols = CHUNK // 16
             return offsets[:, c * cols : (c + 1) * cols]
 
-        zp_picked = staged.tile([P, 2, 4 * P], F32, name="zp_picked", offset=WORDS_AT)
+        big = keep.tile([P, LOW_AT + 4 * S], BF16, name="big")
+        rounded3 = big[:, :T]
+        all_words = big[:, LOW_AT:].rearrange("p (c u s e) -> p c u s e", c=CHUNKS, u=2, e=2)
+        words = [all_words[:, c] for c in range(CHUNKS)]
+        for c in (1, 0):
+            nc.gpsimd.memset(words[c][:, 1].rearrange("p s e -> p (s e)").bitcast(I32), 0)
+
         turneds = []
         for b in range(2):
+            zp_picked = words[2 + b].rearrange("p u s e -> p (u s e)").bitcast(F32)
             for lo, hi in ((0, 512),) if b == 0 else ((0, 256), (256, 512)):
                 first = (512 * b + lo) // 16
-                nc.vector.tensor_copy(zp_picked[:, b, lo:hi], zp_table[:].indirect(offsets[:, first : first + (hi - lo) // 16]))
+                at = (lo + 256 * b) % 512
+                nc.vector.tensor_copy(zp_picked[:, at : at + hi - lo], zp_table[:].indirect(offsets[:, first : first + (hi - lo) // 16]))
             turned = psum.tile([P, 4, P], F32, name=f"turned{b}")
             for c in range(4):
-                nc.tensor.transpose(turned[:, c, :], zp_picked[:, b, c * P : (c + 1) * P], identity[:])
+                at = (c * P + 256 * b) % 512
+                nc.tensor.transpose(turned[:, c, :], zp_picked[:, at : at + P], identity[:])
             turneds.append(turned)
         spreads = []
         for b in range(2):
-            cols = staged.tile([P, 4], F32, name=f"zp_cols{b}", offset=ROUNDED_AT + T * 2 + 32 * b)
+            cols = keep.tile([P, 4], F32, name=f"zp_cols{b}")
             nc.vector.tensor_copy(cols[:], turneds[b][:, :, P - 1])
             spread = psum.tile([P, 4, P], F32, name=f"spread{b}")
             for c in range(4):
                 nc.tensor.transpose(spread[:, c, :], cols[:, c : c + 1].to_broadcast([P, P]), identity[:])
             spreads.append(spread)
 
-        all_words = staged.tile([P, 2, S, 2], BF16, name="all_words", offset=WORDS_AT)
-        words = [all_words[:, :, c * CHUNK : (c + 1) * CHUNK, :] for c in range(CHUNKS)]
-
-        rounded2 = staged.tile([P, T], BF16, name="rounded2", offset=ROUNDED_AT)
-        nc.scalar.copy(rounded2[:, :CAST_SPLIT], planes[2][:, :CAST_SPLIT])
-        nc.vector.tensor_copy(rounded2[:, CAST_SPLIT:], planes[2][:, CAST_SPLIT:])
-        nc.vector.tensor_copy(words[0][:, 1, :, 0], planes[2][:].indirect(entries(0)))
-        nc.scalar.activation(all_words[:, 1, CHUNK:, 0], rounded2[:].indirect(offsets[:, CHUNK // 16 :]), ACT.Copy)
+        rounded2 = keep.tile([P, T], BF16, name="rounded2")
+        nc.scalar.copy(rounded2[:, : T // 2], planes[2][:, : T // 2])
+        nc.gpsimd.tensor_scalar(rounded2[:, T // 2 :], planes[2][:, T // 2 :], 1.0, 0.0, ALU.mult, ALU.add)
+        nc.vector.tensor_copy(words[3][:, 1, :, 0], planes[2][:].indirect(entries(3)))
+        nc.scalar.activation(all_words[:, :3, 1, :, 0], rounded2[:].indirect(offsets[:, : 3 * CHUNK // 16]), ACT.Copy)
 
         picked_zp = staged.tile([P, S], F32, name="picked_zp", offset=PLANE2_AT)
         for b in range(2):
             nc.scalar.copy(picked_zp[:, b * 4 * P : (b + 1) * 4 * P], spreads[b][:].rearrange("p c j -> p (c j)"))
 
-        for t in range(2):
-            nc.vector.tensor_copy(all_words[:, 0, :, t], planes[t][:].indirect(offsets[:]))
-
-        rounded3 = staged.tile([P, T], BF16, name="rounded3", offset=ROUNDED_AT + 64)
-        for lo, hi in LAST_PIECES:
-            nc.scalar.copy(rounded3[:, lo:hi], planes[3][:, lo:hi])
-        nc.vector.tensor_copy(words[0][:, 1, :, 1], planes[3][:].indirect(entries(0)))
-        for c in range(1, CHUNKS):
-            nc.scalar.activation(words[c][:, 1, :, 1], rounded3[:].indirect(entries(c)), ACT.Copy)
+        nc.vector.tensor_copy(all_words[:, :, 0, :, 0], planes[0][:].indirect(offsets[:]))
 
         grouped = {}
         sums = {}
 
-        def join(c):
+        def join(c, on_vector):
             tile = keep.tile([P, CHUNK, 4], BF16, name=f"grouped{c}", tag=f"grouped{c}", align_bytes=64)
-            word = I32 if c < CHUNKS - 1 else U32
-            src = all_words[:].rearrange("p u s e -> p u (s e)").bitcast(word)[:, :, c * CHUNK : (c + 1) * CHUNK]
+            word = I32 if on_vector else U32
+            src = words[c].rearrange("p u s e -> p u (s e)").bitcast(word)
             dst = tile[:].rearrange("p s j -> p (s j)").bitcast(word)
-            src = src.rearrange("p u (g i) -> p g u i", i=RUN)
-            dst = dst.rearrange("p (g i u) -> p g u i", i=RUN, u=2)
-            if c < CHUNKS - 1:
+            src = src.rearrange("p u s -> p s u")
+            dst = dst.rearrange("p (s u) -> p s u", u=2)
+            if on_vector:
                 nc.vector.tensor_copy(dst, src)
             else:
                 nc.scalar.copy(dst, src)
             grouped[c] = tile
+
+        for c in (1, 0):
+            nc.vector.tensor_copy(words[c][:, 0, :, 1], planes[1][:].indirect(entries(c)))
+            join(c, False)
+        nc.vector.tensor_copy(all_words[:, 2:, 0, :, 1], planes[1][:].indirect(offsets[:, S // 32 :]))
+
+        for lo, hi in LAST_PIECES[:3]:
+            nc.gpsimd.tensor_scalar(rounded3[:, lo:hi], planes[3][:, lo:hi], 1.0, 0.0, ALU.mult, ALU.add)
+        for lo, hi in LAST_PIECES[3:]:
+            nc.scalar.copy(rounded3[:, lo:hi], planes[3][:, lo:hi])
+        nc.vector.tensor_copy(words[3][:, 1, :, 1], planes[3][:].indirect(entries(3)))
+        nc.scalar.activation(words[2][:, 1, :, 1], rounded3.indirect(entries(2)), ACT.Copy)
+        for c in (1, 0):
+            nc.scalar.activation(grouped[c][:, :, 3], rounded3.indirect(entries(c)), ACT.Copy)
 
         def multiply(c):
             codes = keep.tile([P, CHUNK], U32, name=f"codes{c}", align_bytes=64)
@@ -152,24 +160,21 @@ def tile_picked_zeropt_gelu_l_kernel(tc, xT, zp, csum, w1_words, w1_scales, offs
 
         def finish(c):
             j0 = c * CHUNK
-            tag = f"grouped{CHUNKS - 1}" if c == 1 else f"shifted{c}"
+            tag = "grouped0" if c == 2 else f"shifted{c}"
             shifted = keep.tile([P, CHUNK], F32, name=f"shifted{c}", tag=tag, align_bytes=64)
             nc.vector.scalar_tensor_tensor(
                 shifted[:], picked_zp[:, j0 : j0 + CHUNK], csum_col[:], sums[c][:], ALU.mult, ALU.subtract
             )
             result = keep.tile([P, CHUNK], F32, name=f"result{c}")
             nc.scalar.activation(result[:], shifted[:], ACT.Gelu_apprx_tanh, scale=-1.0)
-            queue = nc.scalar if c == CHUNKS - 1 else nc.sync
-            queue.dma_start(out[:, j0 : j0 + CHUNK], result[:])
+            nc.sync.dma_start(out[:, j0 : j0 + CHUNK], result[:])
 
-        join(0)
-        join(1)
-        multiply(0)
-        join(2)
-        join(3)
-        multiply(1)
-        multiply(2)
-        finish(0)
+        join(3, True)
+        join(2, True)
         multiply(3)
-        for c in range(1, CHUNKS):
+        multiply(2)
+        multiply(1)
+        finish(3)
+        multiply(0)
+        for c in (2, 1, 0):
             finish(c)

@@ -19,10 +19,8 @@ ACT = mybir.ActivationFunctionType
 ALU = mybir.AluOpType
 
 CHUNK = 256
-CHUNKS = S // CHUNK
-LAST_PIECES = [(0, 512), (512, 1024), (1024, 1536), (1536, 2048)]
-LOW_AT = 1536
-PLANE2_AT = 0
+HALF = S // 2
+PLANE_BYTES = 4 * T
 
 
 def tile_picked_zeropt_gelu_l_kernel(tc, xT, zp, csum, w1_words, w1_scales, offs, out):
@@ -35,21 +33,19 @@ def tile_picked_zeropt_gelu_l_kernel(tc, xT, zp, csum, w1_words, w1_scales, offs
         offsets = keep.tile([P, S // 16], U16, name="offsets")
 
         zp_table = keep.tile([P, T], F32, name="zp_table")
-        nc.vector.memset(zp_table[: P - 1, :], 0.0)
+        nc.vector.memset(zp_table[: P - 1, :].bitcast(I32), 0)
         warm = keep.tile([P, 8], F32, name="warm")
         nc.scalar.activation(warm[32:64, 0:1], zp_table[32:64, 0:1], ACT.Gelu_apprx_tanh)
 
         rows = xT.rearrange("(p j) t -> p j t", j=4)
         planes = [
-            staged.tile([P, T], F32, name="plane2", offset=PLANE2_AT) if t == 2 else keep.tile([P, T], F32, name=f"plane{t}")
+            staged.tile([P, T], F32, name="plane1", offset=0) if t == 1 else keep.tile([P, T], F32, name=f"plane{t}")
             for t in range(4)
         ]
         nc.sync.dma_start(zp_table[P - 1 : P, :], zp[0:1, :])
         nc.sync.dma_start(offsets[:], offs)
-        for t in (2, 0, 1):
+        for t in range(4):
             nc.sync.dma_start(planes[t][:], rows[:, t, :])
-        for lo, hi in LAST_PIECES:
-            nc.sync.dma_start(planes[3][:, lo:hi], rows[:, 3, lo:hi])
 
         w_words = keep.tile([P, 2 * N], U8, name="w_words", align_bytes=64)
         w_scales = keep.tile([P, N], U8, name="w_scales", align_bytes=64)
@@ -66,86 +62,70 @@ def tile_picked_zeropt_gelu_l_kernel(tc, xT, zp, csum, w1_words, w1_scales, offs
         identity = keep.tile([P, P], F32, name="identity")
         make_identity(nc, identity[:])
 
-        def entries(c):
-            cols = CHUNK // 16
-            return offsets[:, c * cols : (c + 1) * cols]
+        def entries(lo, hi):
+            return offsets[:, lo // 16 : hi // 16]
 
-        big = keep.tile([P, LOW_AT + 4 * S], BF16, name="big")
-        rounded3 = big[:, :T]
-        all_words = big[:, LOW_AT:].rearrange("p (c u s e) -> p c u s e", c=CHUNKS, u=2, e=2)
-        words = [all_words[:, c] for c in range(CHUNKS)]
-        for c in (1, 0):
-            nc.gpsimd.memset(words[c][:, 1].rearrange("p s e -> p (s e)").bitcast(I32), 0)
+        direct = keep.tile([P, HALF, 4], BF16, name="direct", align_bytes=64)
+        woven = keep.tile([P, HALF, 4], BF16, name="woven", align_bytes=64)
+        low_rows = keep.tile([P, 2, HALF], BF16, name="low_rows")
 
-        turneds = []
+        zp_picked = keep.tile([P, S], F32, name="zp_picked")
+        turneds = [psum.tile([P, 4, P], F32, name=f"turned{b}") for b in range(2)]
+        for h in range(2):
+            lo = h * CHUNK
+            nc.vector.tensor_copy(zp_picked[:, lo : lo + CHUNK], zp_table[:].indirect(entries(lo, lo + CHUNK)))
+            lo = HALF + h * CHUNK
+            nc.scalar.activation(zp_picked[:, lo : lo + CHUNK], zp_table[:].indirect(entries(lo, lo + CHUNK)), ACT.Copy)
         for b in range(2):
-            zp_picked = words[2 + b].rearrange("p u s e -> p (u s e)").bitcast(F32)
-            for lo, hi in ((0, 512),) if b == 0 else ((0, 256), (256, 512)):
-                first = (512 * b + lo) // 16
-                at = (lo + 256 * b) % 512
-                nc.vector.tensor_copy(zp_picked[:, at : at + hi - lo], zp_table[:].indirect(offsets[:, first : first + (hi - lo) // 16]))
-            turned = psum.tile([P, 4, P], F32, name=f"turned{b}")
-            for c in range(4):
-                at = (c * P + 256 * b) % 512
-                nc.tensor.transpose(turned[:, c, :], zp_picked[:, at : at + P], identity[:])
-            turneds.append(turned)
+            for i in range(4):
+                lo = (4 * b + i) * P
+                nc.tensor.transpose(turneds[b][:, i, :], zp_picked[:, lo : lo + P], identity[:])
         spreads = []
+        all_cols = low_rows[:, 1, :16].bitcast(F32)
         for b in range(2):
-            cols = keep.tile([P, 4], F32, name=f"zp_cols{b}")
-            nc.vector.tensor_copy(cols[:], turneds[b][:, :, P - 1])
+            cols = all_cols[:, 4 * b : 4 * b + 4]
+            nc.scalar.copy(cols, turneds[b][:, :, P - 1])
+            if b == 0:
+                nc.scalar.activation(low_rows[:, 0, CHUNK:], planes[0][:].indirect(entries(HALF + CHUNK, S)), ACT.Copy)
             spread = psum.tile([P, 4, P], F32, name=f"spread{b}")
-            for c in range(4):
-                nc.tensor.transpose(spread[:, c, :], cols[:, c : c + 1].to_broadcast([P, P]), identity[:])
+            for i in range(4):
+                nc.tensor.transpose(spread[:, i, :], cols[:, i : i + 1].to_broadcast([P, P]), identity[:])
             spreads.append(spread)
-
-        rounded2 = keep.tile([P, T], BF16, name="rounded2")
-        nc.scalar.copy(rounded2[:, : T // 2], planes[2][:, : T // 2])
-        nc.gpsimd.tensor_scalar(rounded2[:, T // 2 :], planes[2][:, T // 2 :], 1.0, 0.0, ALU.mult, ALU.add)
-        nc.vector.tensor_copy(words[3][:, 1, :, 0], planes[2][:].indirect(entries(3)))
-        nc.scalar.activation(all_words[:, :3, 1, :, 0], rounded2[:].indirect(offsets[:, : 3 * CHUNK // 16]), ACT.Copy)
-
-        picked_zp = staged.tile([P, S], F32, name="picked_zp", offset=PLANE2_AT)
+        picked_zp = keep.tile([P, S], F32, name="picked_zp")
         for b in range(2):
             nc.scalar.copy(picked_zp[:, b * 4 * P : (b + 1) * 4 * P], spreads[b][:].rearrange("p c j -> p (c j)"))
 
-        nc.vector.tensor_copy(all_words[:, :, 0, :, 0], planes[0][:].indirect(offsets[:]))
+        nc.vector.tensor_copy(direct[:, :, 0], planes[0][:].indirect(entries(0, HALF)))
+        nc.vector.tensor_copy(low_rows[:, 0, :CHUNK], planes[0][:].indirect(entries(HALF, HALF + CHUNK)))
 
-        grouped = {}
+        nc.vector.tensor_copy(direct[:, :, 1], planes[1][:].indirect(entries(0, HALF)))
+        nc.scalar.activation(low_rows[:, 1, :], planes[1][:].indirect(entries(HALF, S)), ACT.Copy)
+        nc.gpsimd.tensor_scalar(woven[:, :, 0:2], low_rows[:].rearrange("p e s -> p s e"), 1.0, 0.0, ALU.mult, ALU.add)
+
+        high_rows = staged.tile([P, 2, HALF], BF16, name="high_rows", offset=0)
+        nc.vector.tensor_copy(direct[:, :, 2], planes[2][:].indirect(entries(0, HALF)))
+        nc.scalar.activation(high_rows[:, 0, :], planes[2][:].indirect(entries(HALF, S)), ACT.Copy)
+
+        for h in range(2):
+            lo = h * CHUNK
+            nc.vector.tensor_copy(direct[:, lo : lo + CHUNK, 3], planes[3][:].indirect(entries(lo, lo + CHUNK)))
+        for h in range(2):
+            lo = h * CHUNK
+            nc.scalar.activation(
+                high_rows[:, 1, lo : lo + CHUNK], planes[3][:].indirect(entries(HALF + lo, HALF + lo + CHUNK)), ACT.Copy
+            )
+        for h in range(2):
+            lo = h * CHUNK
+            nc.scalar.copy(woven[:, lo : lo + CHUNK, 2:4], high_rows[:, :, lo : lo + CHUNK].rearrange("p e s -> p s e"))
+
         sums = {}
 
-        def join(c, on_vector):
-            tile = keep.tile([P, CHUNK, 4], BF16, name=f"grouped{c}", tag=f"grouped{c}", align_bytes=64)
-            word = I32 if on_vector else U32
-            src = words[c].rearrange("p u s e -> p u (s e)").bitcast(word)
-            dst = tile[:].rearrange("p s j -> p (s j)").bitcast(word)
-            src = src.rearrange("p u s -> p s u")
-            dst = dst.rearrange("p (s u) -> p s u", u=2)
-            if on_vector:
-                nc.vector.tensor_copy(dst, src)
-            else:
-                nc.scalar.copy(dst, src)
-            grouped[c] = tile
-
-        for c in (1, 0):
-            nc.vector.tensor_copy(words[c][:, 0, :, 1], planes[1][:].indirect(entries(c)))
-            join(c, False)
-        nc.vector.tensor_copy(all_words[:, 2:, 0, :, 1], planes[1][:].indirect(offsets[:, S // 32 :]))
-
-        for lo, hi in LAST_PIECES[:3]:
-            nc.gpsimd.tensor_scalar(rounded3[:, lo:hi], planes[3][:, lo:hi], 1.0, 0.0, ALU.mult, ALU.add)
-        for lo, hi in LAST_PIECES[3:]:
-            nc.scalar.copy(rounded3[:, lo:hi], planes[3][:, lo:hi])
-        nc.vector.tensor_copy(words[3][:, 1, :, 1], planes[3][:].indirect(entries(3)))
-        nc.scalar.activation(words[2][:, 1, :, 1], rounded3.indirect(entries(2)), ACT.Copy)
-        for c in (1, 0):
-            nc.scalar.activation(grouped[c][:, :, 3], rounded3.indirect(entries(c)), ACT.Copy)
-
         def multiply(c):
+            lo = (c % 2) * CHUNK
+            grouped = (direct, woven)[c // 2][:, lo : lo + CHUNK, :]
             codes = keep.tile([P, CHUNK], U32, name=f"codes{c}", align_bytes=64)
             scales = keep.tile([P, CHUNK], U8, name=f"scales{c}", align_bytes=64)
-            nc.vector.quantize_mx(
-                out=codes[:].bitcast(FP8X4), scales=scales[:], in_=grouped[c][:].rearrange("p s j -> p (s j)")
-            )
+            nc.vector.quantize_mx(out=codes[:].bitcast(FP8X4), scales=scales[:], in_=grouped.rearrange("p s j -> p (s j)"))
             acc = psum.tile([P, CHUNK], F32, name=f"acc{c}")
             nc.tensor.matmul_mx(
                 out=acc[:],
@@ -160,8 +140,7 @@ def tile_picked_zeropt_gelu_l_kernel(tc, xT, zp, csum, w1_words, w1_scales, offs
 
         def finish(c):
             j0 = c * CHUNK
-            tag = "grouped0" if c == 2 else f"shifted{c}"
-            shifted = keep.tile([P, CHUNK], F32, name=f"shifted{c}", tag=tag, align_bytes=64)
+            shifted = keep.tile([P, CHUNK], F32, name=f"shifted{c}", align_bytes=64)
             nc.vector.scalar_tensor_tensor(
                 shifted[:], picked_zp[:, j0 : j0 + CHUNK], csum_col[:], sums[c][:], ALU.mult, ALU.subtract
             )
@@ -169,12 +148,11 @@ def tile_picked_zeropt_gelu_l_kernel(tc, xT, zp, csum, w1_words, w1_scales, offs
             nc.scalar.activation(result[:], shifted[:], ACT.Gelu_apprx_tanh, scale=-1.0)
             nc.sync.dma_start(out[:, j0 : j0 + CHUNK], result[:])
 
-        join(3, True)
-        join(2, True)
-        multiply(3)
-        multiply(2)
-        multiply(1)
-        finish(3)
         multiply(0)
-        for c in (2, 1, 0):
-            finish(c)
+        multiply(1)
+        multiply(2)
+        finish(0)
+        finish(1)
+        multiply(3)
+        finish(2)
+        finish(3)

@@ -114,9 +114,10 @@ def tile_picked_zeropt_gelu_l_kernel(tc, xT, zp, csum, w1_words, w1_scales, offs
             nc.scalar.activation(
                 high_rows[:, 1, lo : lo + CHUNK], planes[3][:].indirect(entries(HALF + lo, HALF + lo + CHUNK)), ACT.Copy
             )
-        for h in range(2):
-            lo = h * CHUNK
-            nc.scalar.copy(woven[:, lo : lo + CHUNK, 2:4], high_rows[:, :, lo : lo + CHUNK].rearrange("p e s -> p s e"))
+        nc.gpsimd.tensor_scalar(
+            woven[:, :CHUNK, 2:4], high_rows[:, :, :CHUNK].rearrange("p e s -> p s e"), 1.0, 0.0, ALU.mult, ALU.add
+        )
+        nc.scalar.copy(woven[:, CHUNK:, 2:4], high_rows[:, :, CHUNK:].rearrange("p e s -> p s e"))
 
         sums = {}
 

@@ -32,6 +32,8 @@ def tile_picked_zeropt_gelu_l_kernel(tc, xT, zp, csum, w1_words, w1_scales, offs
 
         offsets = keep.tile([P, S // 16], U16, name="offsets")
 
+        w_scales = keep.tile([P, N], U8, name="w_scales", align_bytes=64)
+        nc.vector.memset(w_scales[:].bitcast(I32), 0)
         zp_table = keep.tile([P, T], F32, name="zp_table")
         nc.vector.memset(zp_table[: P - 1, :].bitcast(I32), 0)
         warm = keep.tile([P, 8], F32, name="warm")
@@ -48,16 +50,14 @@ def tile_picked_zeropt_gelu_l_kernel(tc, xT, zp, csum, w1_words, w1_scales, offs
             nc.sync.dma_start(planes[t][:], rows[:, t, :])
 
         w_words = keep.tile([P, 2 * N], U8, name="w_words", align_bytes=64)
-        w_scales = keep.tile([P, N], U8, name="w_scales", align_bytes=64)
         csum_col = keep.tile([P, 1], F32, name="csum_col")
-        nc.sync.dma_start(csum_col[:], csum)
         nc.sync.dma_start(w_words[:].bitcast(I32), w1_words[0].bitcast(I32))
-        nc.vector.memset(w_scales[:].bitcast(I32), 0)
         for q in range(4):
             nc.sync.dma_start(
                 w_scales[32 * q : 32 * q + 4, :].bitcast(I32),
                 w1_scales[0, 4 * q : 4 * q + 4, :].bitcast(I32),
             )
+        nc.sync.dma_start(csum_col[:], csum)
 
         identity = keep.tile([P, P], F32, name="identity")
         make_identity(nc, identity[:])
@@ -141,7 +141,10 @@ def tile_picked_zeropt_gelu_l_kernel(tc, xT, zp, csum, w1_words, w1_scales, offs
 
         def finish(c):
             j0 = c * CHUNK
-            shifted = keep.tile([P, CHUNK], F32, name=f"shifted{c}", align_bytes=64)
+            if c == 0:
+                shifted = staged.tile([P, CHUNK], F32, name="shifted0", offset=0)
+            else:
+                shifted = keep.tile([P, CHUNK], F32, name=f"shifted{c}")
             nc.vector.scalar_tensor_tensor(
                 shifted[:], picked_zp[:, j0 : j0 + CHUNK], csum_col[:], sums[c][:], ALU.mult, ALU.subtract
             )
@@ -149,11 +152,7 @@ def tile_picked_zeropt_gelu_l_kernel(tc, xT, zp, csum, w1_words, w1_scales, offs
             nc.scalar.activation(result[:], shifted[:], ACT.Gelu_apprx_tanh, scale=-1.0)
             nc.sync.dma_start(out[:, j0 : j0 + CHUNK], result[:])
 
-        multiply(0)
-        multiply(1)
-        multiply(2)
-        finish(0)
-        finish(1)
-        multiply(3)
-        finish(2)
-        finish(3)
+        for c in range(4):
+            multiply(c)
+        for c in range(4):
+            finish(c)

@@ -20,7 +20,11 @@ ALU = mybir.AluOpType
 
 CHUNK = 256
 HALF = S // 2
-PLANE_BYTES = 4 * T
+DIRECT = 480
+WOVEN = S - DIRECT
+EARLY = 224
+LATE_AT = 1024
+STRETCHES = [(512, 640), (0, 256), (256, 512), (640, 896), (896, 1024)]
 
 
 def tile_picked_zeropt_gelu_l_kernel(tc, xT, zp, csum, w1_words, w1_scales, offs, out):
@@ -65,9 +69,10 @@ def tile_picked_zeropt_gelu_l_kernel(tc, xT, zp, csum, w1_words, w1_scales, offs
         def entries(lo, hi):
             return offsets[:, lo // 16 : hi // 16]
 
-        direct = keep.tile([P, HALF, 4], BF16, name="direct", align_bytes=64)
-        woven = keep.tile([P, HALF, 4], BF16, name="woven", align_bytes=64)
-        low_rows = keep.tile([P, 2, HALF], BF16, name="low_rows")
+        grouped = keep.tile([P, S, 4], BF16, name="grouped", align_bytes=64)
+        direct = grouped[:, :DIRECT]
+        woven = grouped[:, DIRECT:]
+        low_rows = keep.tile([P, 2, WOVEN], BF16, name="low_rows")
 
         zp_picked = keep.tile([P, S], F32, name="zp_picked")
         turneds = [psum.tile([P, 4, P], F32, name=f"turned{b}") for b in range(2)]
@@ -86,7 +91,7 @@ def tile_picked_zeropt_gelu_l_kernel(tc, xT, zp, csum, w1_words, w1_scales, offs
             cols = all_cols[:, 4 * b : 4 * b + 4]
             nc.scalar.copy(cols, turneds[b][:, :, P - 1])
             if b == 0:
-                nc.scalar.activation(low_rows[:, 0, CHUNK:], planes[0][:].indirect(entries(HALF + CHUNK, S)), ACT.Copy)
+                nc.scalar.activation(low_rows[:, 0, CHUNK:], planes[0][:].indirect(entries(DIRECT + CHUNK, S)), ACT.Copy)
             spread = psum.tile([P, 4, P], F32, name=f"spread{b}")
             for i in range(4):
                 nc.tensor.transpose(spread[:, i, :], cols[:, i : i + 1].to_broadcast([P, P]), identity[:])
@@ -95,39 +100,45 @@ def tile_picked_zeropt_gelu_l_kernel(tc, xT, zp, csum, w1_words, w1_scales, offs
         for b in range(2):
             nc.scalar.copy(picked_zp[:, b * 4 * P : (b + 1) * 4 * P], spreads[b][:].rearrange("p c j -> p (c j)"))
 
-        nc.vector.tensor_copy(direct[:, :, 0], planes[0][:].indirect(entries(0, HALF)))
-        nc.vector.tensor_copy(low_rows[:, 0, :CHUNK], planes[0][:].indirect(entries(HALF, HALF + CHUNK)))
+        nc.vector.tensor_copy(direct[:, :, 0], planes[0][:].indirect(entries(0, DIRECT)))
+        nc.vector.tensor_copy(low_rows[:, 0, :CHUNK], planes[0][:].indirect(entries(DIRECT, DIRECT + CHUNK)))
 
-        nc.vector.tensor_copy(direct[:, :, 1], planes[1][:].indirect(entries(0, HALF)))
-        nc.scalar.activation(low_rows[:, 1, :], planes[1][:].indirect(entries(HALF, S)), ACT.Copy)
+        nc.vector.tensor_copy(direct[:, :, 1], planes[1][:].indirect(entries(0, DIRECT)))
+        nc.scalar.activation(low_rows[:, 1, :], planes[1][:].indirect(entries(DIRECT, S)), ACT.Copy)
         nc.gpsimd.tensor_scalar(woven[:, :, 0:2], low_rows[:].rearrange("p e s -> p s e"), 1.0, 0.0, ALU.mult, ALU.add)
 
-        high_rows = staged.tile([P, 2, HALF], BF16, name="high_rows", offset=0)
-        nc.vector.tensor_copy(direct[:, :, 2], planes[2][:].indirect(entries(0, HALF)))
-        nc.scalar.activation(high_rows[:, 0, :], planes[2][:].indirect(entries(HALF, S)), ACT.Copy)
+        early_rows = staged.tile([P, 2, EARLY], BF16, name="early_rows", offset=0)
+        late_rows = staged.tile([P, 2, WOVEN - EARLY], BF16, name="late_rows", offset=LATE_AT)
+        late = DIRECT + EARLY
+        nc.vector.tensor_copy(direct[:, :, 2], planes[2][:].indirect(entries(0, DIRECT)))
+        nc.scalar.activation(early_rows[:, 0, :], planes[2][:].indirect(entries(DIRECT, late)), ACT.Copy)
+        nc.scalar.activation(late_rows[:, 0, :], planes[2][:].indirect(entries(late, S)), ACT.Copy)
 
-        for h in range(2):
-            lo = h * CHUNK
-            nc.vector.tensor_copy(direct[:, lo : lo + CHUNK, 3], planes[3][:].indirect(entries(lo, lo + CHUNK)))
-        for h in range(2):
-            lo = h * CHUNK
-            nc.scalar.activation(
-                high_rows[:, 1, lo : lo + CHUNK], planes[3][:].indirect(entries(HALF + lo, HALF + lo + CHUNK)), ACT.Copy
-            )
+        nc.vector.tensor_copy(direct[:, :, 3], planes[3][:].indirect(entries(0, DIRECT)))
+        nc.scalar.activation(early_rows[:, 1, :], planes[3][:].indirect(entries(DIRECT, late)), ACT.Copy)
+        pieces = ((late, 896), (896, S))
+        for lo, hi in pieces:
+            nc.scalar.activation(late_rows[:, 1, lo - late : hi - late], planes[3][:].indirect(entries(lo, hi)), ACT.Copy)
         nc.gpsimd.tensor_scalar(
-            woven[:, :CHUNK, 2:4], high_rows[:, :, :CHUNK].rearrange("p e s -> p s e"), 1.0, 0.0, ALU.mult, ALU.add
+            grouped[:, DIRECT:late, 2:4], early_rows[:].rearrange("p e s -> p s e"), 1.0, 0.0, ALU.mult, ALU.add
         )
-        nc.scalar.copy(woven[:, CHUNK:, 2:4], high_rows[:, :, CHUNK:].rearrange("p e s -> p s e"))
+        for lo, hi in pieces:
+            nc.scalar.copy(grouped[:, lo:hi, 2:4], late_rows[:, :, lo - late : hi - late].rearrange("p e s -> p s e"))
 
         sums = {}
+        shifted = staged.tile([P, S], F32, name="shifted", offset=LATE_AT)
 
         def multiply(c):
-            lo = (c % 2) * CHUNK
-            grouped = (direct, woven)[c // 2][:, lo : lo + CHUNK, :]
-            codes = keep.tile([P, CHUNK], U32, name=f"codes{c}", align_bytes=64)
-            scales = keep.tile([P, CHUNK], U8, name=f"scales{c}", align_bytes=64)
-            nc.vector.quantize_mx(out=codes[:].bitcast(FP8X4), scales=scales[:], in_=grouped.rearrange("p s j -> p (s j)"))
-            acc = psum.tile([P, CHUNK], F32, name=f"acc{c}")
+            lo, hi = STRETCHES[c]
+            if c == 1:
+                codes = staged.tile([P, hi - lo], U32, name="codes1", align_bytes=64, offset=0)
+            else:
+                codes = keep.tile([P, hi - lo], U32, name=f"codes{c}", align_bytes=64)
+            scales = keep.tile([P, hi - lo], U8, name=f"scales{c}", align_bytes=64)
+            nc.vector.quantize_mx(
+                out=codes[:].bitcast(FP8X4), scales=scales[:], in_=grouped[:, lo:hi].rearrange("p s j -> p (s j)")
+            )
+            acc = psum.tile([P, hi - lo], F32, name=f"acc{c}", tag="turned0" if c == 4 else f"acc{c}")
             nc.tensor.matmul_mx(
                 out=acc[:],
                 lhsT=w_words[:].bitcast(FP4X4),
@@ -140,19 +151,15 @@ def tile_picked_zeropt_gelu_l_kernel(tc, xT, zp, csum, w1_words, w1_scales, offs
             sums[c] = acc
 
         def finish(c):
-            j0 = c * CHUNK
-            if c == 0:
-                shifted = staged.tile([P, CHUNK], F32, name="shifted0", offset=0)
-            else:
-                shifted = keep.tile([P, CHUNK], F32, name=f"shifted{c}")
+            lo, hi = STRETCHES[c]
             nc.vector.scalar_tensor_tensor(
-                shifted[:], picked_zp[:, j0 : j0 + CHUNK], csum_col[:], sums[c][:], ALU.mult, ALU.subtract
+                shifted[:, lo:hi], picked_zp[:, lo:hi], csum_col[:], sums[c][:], ALU.mult, ALU.subtract
             )
-            result = keep.tile([P, CHUNK], F32, name=f"result{c}")
-            nc.scalar.activation(result[:], shifted[:], ACT.Gelu_apprx_tanh, scale=-1.0)
-            nc.sync.dma_start(out[:, j0 : j0 + CHUNK], result[:])
+            result = keep.tile([P, hi - lo], F32, name=f"result{c}")
+            nc.scalar.activation(result[:], shifted[:, lo:hi], ACT.Gelu_apprx_tanh, scale=-1.0)
+            nc.sync.dma_start(out[:, lo:hi], result[:])
 
-        for c in range(4):
+        for c in range(len(STRETCHES)):
             multiply(c)
-        for c in range(4):
+        for c in range(len(STRETCHES)):
             finish(c)

@@ -19,33 +19,42 @@ ACT = mybir.ActivationFunctionType
 ALU = mybir.AluOpType
 
 CHUNK = 256
-HALF = S // 2
-DIRECT = 480
+CHUNKS = S // CHUNK
+BANK = 512
+LIST_ROWS = 16
+
+DIRECT = 544
+EARLY = 256
+LATE = DIRECT + EARLY
 WOVEN = S - DIRECT
-EARLY = 224
-LATE_AT = 1024
-STRETCHES = [(512, 640), (0, 256), (256, 512), (640, 896), (896, 1024)]
+VECTOR_ROWS = 256
+LATE_ROWS_AT = 2 * 2 * EARLY
 
 
 def tile_picked_zeropt_gelu_l_kernel(tc, xT, zp, csum, w1_words, w1_scales, offs, out):
     nc = tc.nc
     with ExitStack() as ctx:
         keep = ctx.enter_context(tc.tile_pool(name="keep", bufs=1))
-        staged = ctx.enter_context(tc.tile_pool(name="staged", bufs=1))
+        reused = ctx.enter_context(tc.tile_pool(name="reused", bufs=1))
         psum = ctx.enter_context(tc.psum_pool(name="psum", bufs=1))
 
-        offsets = keep.tile([P, S // 16], U16, name="offsets")
+        offsets = keep.tile([P, S // LIST_ROWS], U16, name="offsets")
+
+        def entries(lo, hi):
+            return offsets[:, lo // LIST_ROWS : hi // LIST_ROWS]
+
+        warm = keep.tile([P, 2], F32, name="warm")
+        nc.vector.memset(warm[:, 0:1], 0.0)
+        nc.scalar.activation(warm[:, 1:2], warm[:, 0:1], ACT.Gelu_apprx_tanh)
 
         w_scales = keep.tile([P, N], U8, name="w_scales", align_bytes=64)
         nc.vector.memset(w_scales[:].bitcast(I32), 0)
         zp_table = keep.tile([P, T], F32, name="zp_table")
         nc.vector.memset(zp_table[: P - 1, :].bitcast(I32), 0)
-        warm = keep.tile([P, 8], F32, name="warm")
-        nc.scalar.activation(warm[32:64, 0:1], zp_table[32:64, 0:1], ACT.Gelu_apprx_tanh)
 
-        rows = xT.rearrange("(p j) t -> p j t", j=4)
+        rows = xT.rearrange("(p t) c -> p t c", t=4)
         planes = [
-            staged.tile([P, T], F32, name="plane1", offset=0) if t == 1 else keep.tile([P, T], F32, name=f"plane{t}")
+            reused.tile([P, T], F32, name="plane1", offset=0) if t == 1 else keep.tile([P, T], F32, name=f"plane{t}")
             for t in range(4)
         ]
         nc.sync.dma_start(zp_table[P - 1 : P, :], zp[0:1, :])
@@ -66,79 +75,70 @@ def tile_picked_zeropt_gelu_l_kernel(tc, xT, zp, csum, w1_words, w1_scales, offs
         identity = keep.tile([P, P], F32, name="identity")
         make_identity(nc, identity[:])
 
-        def entries(lo, hi):
-            return offsets[:, lo // 16 : hi // 16]
-
         grouped = keep.tile([P, S, 4], BF16, name="grouped", align_bytes=64)
-        direct = grouped[:, :DIRECT]
-        woven = grouped[:, DIRECT:]
         low_rows = keep.tile([P, 2, WOVEN], BF16, name="low_rows")
 
-        zp_picked = keep.tile([P, S], F32, name="zp_picked")
-        turneds = [psum.tile([P, 4, P], F32, name=f"turned{b}") for b in range(2)]
+        def weave_source(two_rows):
+            return two_rows.rearrange("p e j -> p j e")
+
+        zp_row = keep.tile([P, S], F32, name="zp_row")
+        turned = [psum.tile([P, 4, P], F32, name=f"turned{b}") for b in range(2)]
         for h in range(2):
             lo = h * CHUNK
-            nc.vector.tensor_copy(zp_picked[:, lo : lo + CHUNK], zp_table[:].indirect(entries(lo, lo + CHUNK)))
-            lo = HALF + h * CHUNK
-            nc.scalar.activation(zp_picked[:, lo : lo + CHUNK], zp_table[:].indirect(entries(lo, lo + CHUNK)), ACT.Copy)
+            nc.vector.tensor_copy(zp_row[:, lo : lo + CHUNK], zp_table[:].indirect(entries(lo, lo + CHUNK)))
+            lo = S // 2 + h * CHUNK
+            nc.scalar.activation(zp_row[:, lo : lo + CHUNK], zp_table[:].indirect(entries(lo, lo + CHUNK)), ACT.Copy)
         for b in range(2):
             for i in range(4):
-                lo = (4 * b + i) * P
-                nc.tensor.transpose(turneds[b][:, i, :], zp_picked[:, lo : lo + P], identity[:])
-        spreads = []
-        all_cols = low_rows[:, 1, :16].bitcast(F32)
+                lo = b * BANK + i * P
+                nc.tensor.transpose(turned[b][:, i, :], zp_row[:, lo : lo + P], identity[:])
+        zp_cols = low_rows[:, 1, :16].bitcast(F32)
+        spread = []
         for b in range(2):
-            cols = all_cols[:, 4 * b : 4 * b + 4]
-            nc.scalar.copy(cols, turneds[b][:, :, P - 1])
+            cols = zp_cols[:, 4 * b : 4 * b + 4]
+            nc.scalar.copy(cols, turned[b][:, :, P - 1])
             if b == 0:
-                nc.scalar.activation(low_rows[:, 0, CHUNK:], planes[0][:].indirect(entries(DIRECT + CHUNK, S)), ACT.Copy)
-            spread = psum.tile([P, 4, P], F32, name=f"spread{b}")
+                nc.scalar.activation(
+                    low_rows[:, 0, VECTOR_ROWS:], planes[0][:].indirect(entries(DIRECT + VECTOR_ROWS, S)), ACT.Copy
+                )
+            bank = psum.tile([P, 4, P], F32, name=f"spread{b}")
             for i in range(4):
-                nc.tensor.transpose(spread[:, i, :], cols[:, i : i + 1].to_broadcast([P, P]), identity[:])
-            spreads.append(spread)
-        picked_zp = keep.tile([P, S], F32, name="picked_zp")
+                nc.tensor.transpose(bank[:, i, :], cols[:, i : i + 1].to_broadcast([P, P]), identity[:])
+            spread.append(bank)
+        zp_picked = keep.tile([P, S], F32, name="zp_picked")
         for b in range(2):
-            nc.scalar.copy(picked_zp[:, b * 4 * P : (b + 1) * 4 * P], spreads[b][:].rearrange("p c j -> p (c j)"))
+            nc.scalar.copy(zp_picked[:, b * BANK : (b + 1) * BANK], spread[b][:].rearrange("p i j -> p (i j)"))
 
-        nc.vector.tensor_copy(direct[:, :, 0], planes[0][:].indirect(entries(0, DIRECT)))
-        nc.vector.tensor_copy(low_rows[:, 0, :CHUNK], planes[0][:].indirect(entries(DIRECT, DIRECT + CHUNK)))
-
-        nc.vector.tensor_copy(direct[:, :, 1], planes[1][:].indirect(entries(0, DIRECT)))
+        nc.vector.tensor_copy(grouped[:, :DIRECT, 0], planes[0][:].indirect(entries(0, DIRECT)))
+        nc.vector.tensor_copy(low_rows[:, 0, :VECTOR_ROWS], planes[0][:].indirect(entries(DIRECT, DIRECT + VECTOR_ROWS)))
+        nc.vector.tensor_copy(grouped[:, :DIRECT, 1], planes[1][:].indirect(entries(0, DIRECT)))
         nc.scalar.activation(low_rows[:, 1, :], planes[1][:].indirect(entries(DIRECT, S)), ACT.Copy)
-        nc.gpsimd.tensor_scalar(woven[:, :, 0:2], low_rows[:].rearrange("p e s -> p s e"), 1.0, 0.0, ALU.mult, ALU.add)
+        nc.gpsimd.tensor_scalar(grouped[:, DIRECT:, 0:2], weave_source(low_rows[:]), 1.0, 0.0, ALU.mult, ALU.add)
 
-        early_rows = staged.tile([P, 2, EARLY], BF16, name="early_rows", offset=0)
-        late_rows = staged.tile([P, 2, WOVEN - EARLY], BF16, name="late_rows", offset=LATE_AT)
-        late = DIRECT + EARLY
-        nc.vector.tensor_copy(direct[:, :, 2], planes[2][:].indirect(entries(0, DIRECT)))
-        nc.scalar.activation(early_rows[:, 0, :], planes[2][:].indirect(entries(DIRECT, late)), ACT.Copy)
-        nc.scalar.activation(late_rows[:, 0, :], planes[2][:].indirect(entries(late, S)), ACT.Copy)
+        early_rows = reused.tile([P, 2, EARLY], BF16, name="early_rows", offset=0)
+        late_rows = reused.tile([P, 2, S - LATE], BF16, name="late_rows", offset=LATE_ROWS_AT)
+        nc.vector.tensor_copy(grouped[:, :DIRECT, 2], planes[2][:].indirect(entries(0, DIRECT)))
+        nc.scalar.activation(early_rows[:, 0, :], planes[2][:].indirect(entries(DIRECT, LATE)), ACT.Copy)
+        nc.scalar.activation(late_rows[:, 0, :], planes[2][:].indirect(entries(LATE, S)), ACT.Copy)
 
-        nc.vector.tensor_copy(direct[:, :, 3], planes[3][:].indirect(entries(0, DIRECT)))
-        nc.scalar.activation(early_rows[:, 1, :], planes[3][:].indirect(entries(DIRECT, late)), ACT.Copy)
-        pieces = ((late, 896), (896, S))
-        for lo, hi in pieces:
-            nc.scalar.activation(late_rows[:, 1, lo - late : hi - late], planes[3][:].indirect(entries(lo, hi)), ACT.Copy)
-        nc.gpsimd.tensor_scalar(
-            grouped[:, DIRECT:late, 2:4], early_rows[:].rearrange("p e s -> p s e"), 1.0, 0.0, ALU.mult, ALU.add
-        )
-        for lo, hi in pieces:
-            nc.scalar.copy(grouped[:, lo:hi, 2:4], late_rows[:, :, lo - late : hi - late].rearrange("p e s -> p s e"))
+        for lo, hi in ((0, CHUNK), (CHUNK, DIRECT)):
+            nc.vector.tensor_copy(grouped[:, lo:hi, 3], planes[3][:].indirect(entries(lo, hi)))
+        nc.scalar.activation(early_rows[:, 1, :], planes[3][:].indirect(entries(DIRECT, LATE)), ACT.Copy)
+        nc.scalar.activation(late_rows[:, 1, :], planes[3][:].indirect(entries(LATE, S)), ACT.Copy)
+        nc.gpsimd.tensor_scalar(grouped[:, DIRECT:LATE, 2:4], weave_source(early_rows[:]), 1.0, 0.0, ALU.mult, ALU.add)
+        nc.scalar.copy(grouped[:, LATE:, 2:4], weave_source(late_rows[:]))
 
-        sums = {}
-        shifted = staged.tile([P, S], F32, name="shifted", offset=LATE_AT)
-
-        def multiply(c):
-            lo, hi = STRETCHES[c]
-            if c == 1:
-                codes = staged.tile([P, hi - lo], U32, name="codes1", align_bytes=64, offset=0)
-            else:
-                codes = keep.tile([P, hi - lo], U32, name=f"codes{c}", align_bytes=64)
-            scales = keep.tile([P, hi - lo], U8, name=f"scales{c}", align_bytes=64)
+        negated = reused.tile([P, S], F32, name="negated", offset=LATE_ROWS_AT)
+        sums = []
+        for c in range(CHUNKS):
+            codes = keep.tile([P, CHUNK], U32, name=f"codes{c}", align_bytes=64)
+            scales = keep.tile([P, CHUNK], U8, name=f"scales{c}", align_bytes=64)
             nc.vector.quantize_mx(
-                out=codes[:].bitcast(FP8X4), scales=scales[:], in_=grouped[:, lo:hi].rearrange("p s j -> p (s j)")
+                out=codes[:].bitcast(FP8X4),
+                scales=scales[:],
+                in_=grouped[:, c * CHUNK : (c + 1) * CHUNK].rearrange("p j t -> p (j t)"),
             )
-            acc = psum.tile([P, hi - lo], F32, name=f"acc{c}", tag="turned0" if c == 4 else f"acc{c}")
+            acc = psum.tile([P, CHUNK], F32, name=f"acc{c}")
             nc.tensor.matmul_mx(
                 out=acc[:],
                 lhsT=w_words[:].bitcast(FP4X4),
@@ -148,18 +148,13 @@ def tile_picked_zeropt_gelu_l_kernel(tc, xT, zp, csum, w1_words, w1_scales, offs
                 start=True,
                 stop=True,
             )
-            sums[c] = acc
+            sums.append(acc)
 
-        def finish(c):
-            lo, hi = STRETCHES[c]
+        for c in range(CHUNKS):
+            chunk = slice(c * CHUNK, (c + 1) * CHUNK)
             nc.vector.scalar_tensor_tensor(
-                shifted[:, lo:hi], picked_zp[:, lo:hi], csum_col[:], sums[c][:], ALU.mult, ALU.subtract
+                negated[:, chunk], zp_picked[:, chunk], csum_col[:], sums[c][:], ALU.mult, ALU.subtract
             )
-            result = keep.tile([P, hi - lo], F32, name=f"result{c}")
-            nc.scalar.activation(result[:], shifted[:, lo:hi], ACT.Gelu_apprx_tanh, scale=-1.0)
-            nc.sync.dma_start(out[:, lo:hi], result[:])
-
-        for c in range(len(STRETCHES)):
-            multiply(c)
-        for c in range(len(STRETCHES)):
-            finish(c)
+            result = keep.tile([P, CHUNK], F32, name=f"result{c}")
+            nc.scalar.activation(result[:], negated[:, chunk], ACT.Gelu_apprx_tanh, scale=-1.0)
+            nc.sync.dma_start(out[:, chunk], result[:])

@@ -20,15 +20,15 @@ ALU = mybir.AluOpType
 
 CHUNK = 256
 CHUNKS = S // CHUNK
-BANK = 512
 LIST_ROWS = 16
+ZP_COLS = T // P
 
-DIRECT = 544
-EARLY = 256
-LATE = DIRECT + EARLY
+DIRECT = 512
 WOVEN = S - DIRECT
-VECTOR_ROWS = 256
-LATE_ROWS_AT = 2 * 2 * EARLY
+POOL_RUN = (S - 192, S)
+SCALAR_RUNS = ((672, 832), (512, 672))
+LOW_DIRECT = 704
+CHUNK_ORDER = (0, 1, 3, 2)
 
 
 def tile_picked_zeropt_gelu_l_kernel(tc, xT, zp, csum, w1_words, w1_scales, offs, out):
@@ -49,17 +49,14 @@ def tile_picked_zeropt_gelu_l_kernel(tc, xT, zp, csum, w1_words, w1_scales, offs
 
         w_scales = keep.tile([P, N], U8, name="w_scales", align_bytes=64)
         nc.vector.memset(w_scales[:].bitcast(I32), 0)
-        zp_table = keep.tile([P, T], F32, name="zp_table")
-        nc.vector.memset(zp_table[: P - 1, :].bitcast(I32), 0)
 
         rows = xT.rearrange("(p t) c -> p t c", t=4)
-        planes = [
-            reused.tile([P, T], F32, name="plane1", offset=0) if t == 1 else keep.tile([P, T], F32, name=f"plane{t}")
-            for t in range(4)
-        ]
-        nc.sync.dma_start(zp_table[P - 1 : P, :], zp[0:1, :])
+        planes = [keep.tile([P, T], F32, name=f"plane{t}") for t in range(4)]
+        zp_dealt = keep.tile([P, ZP_COLS], F32, name="zp_dealt")
+        nc.sync.dma_start(zp_dealt[:], zp[0].rearrange("(p i) -> p i", i=ZP_COLS))
+        nc.sync.dma_start(planes[0][:], rows[:, 0, :])
         nc.sync.dma_start(offsets[:], offs)
-        for t in range(4):
+        for t in range(1, 4):
             nc.sync.dma_start(planes[t][:], rows[:, t, :])
 
         w_words = keep.tile([P, 2 * N], U8, name="w_words", align_bytes=64)
@@ -76,61 +73,52 @@ def tile_picked_zeropt_gelu_l_kernel(tc, xT, zp, csum, w1_words, w1_scales, offs
         make_identity(nc, identity[:])
 
         grouped = keep.tile([P, S, 4], BF16, name="grouped", align_bytes=64)
-        low_rows = keep.tile([P, 2, WOVEN], BF16, name="low_rows")
 
-        def weave_source(two_rows):
-            return two_rows.rearrange("p e j -> p j e")
+        def direct(t, lo, hi):
+            nc.vector.tensor_copy(grouped[:, lo:hi, t], planes[t][:].indirect(entries(lo, hi)))
 
-        zp_row = keep.tile([P, S], F32, name="zp_row")
-        turned = [psum.tile([P, 4, P], F32, name=f"turned{b}") for b in range(2)]
-        for h in range(2):
-            lo = h * CHUNK
-            nc.vector.tensor_copy(zp_row[:, lo : lo + CHUNK], zp_table[:].indirect(entries(lo, lo + CHUNK)))
-            lo = S // 2 + h * CHUNK
-            nc.scalar.activation(zp_row[:, lo : lo + CHUNK], zp_table[:].indirect(entries(lo, lo + CHUNK)), ACT.Copy)
-        for b in range(2):
-            for i in range(4):
-                lo = b * BANK + i * P
-                nc.tensor.transpose(turned[b][:, i, :], zp_row[:, lo : lo + P], identity[:])
-        zp_cols = low_rows[:, 1, :16].bitcast(F32)
-        spread = []
-        for b in range(2):
-            cols = zp_cols[:, 4 * b : 4 * b + 4]
-            nc.scalar.copy(cols, turned[b][:, :, P - 1])
-            if b == 0:
-                nc.scalar.activation(
-                    low_rows[:, 0, VECTOR_ROWS:], planes[0][:].indirect(entries(DIRECT + VECTOR_ROWS, S)), ACT.Copy
-                )
+        def to_row(two_rows, t, lo, hi):
+            nc.scalar.activation(
+                two_rows[:, t % 2, lo - DIRECT : hi - DIRECT], planes[t][:].indirect(entries(lo, hi)), ACT.Copy
+            )
+
+        def weave_views(two_rows, first_t, lo, hi):
+            source = two_rows[:, :, lo - DIRECT : hi - DIRECT].rearrange("p e j -> p j e")
+            return grouped[:, lo:hi, first_t : first_t + 2], source
+
+        zp_table = reused.tile([P, T], F32, name="zp_table", offset=0)
+        table_by_bank = zp_table[:].rearrange("p (n b i) -> p b n i", b=4, i=4)
+        for b in range(4):
             bank = psum.tile([P, 4, P], F32, name=f"spread{b}")
             for i in range(4):
-                nc.tensor.transpose(bank[:, i, :], cols[:, i : i + 1].to_broadcast([P, P]), identity[:])
-            spread.append(bank)
+                col = 4 * b + i
+                nc.tensor.transpose(bank[:, i, :], zp_dealt[:, col : col + 1].to_broadcast([P, P]), identity[:])
+            nc.scalar.copy(table_by_bank[:, b], bank[:].rearrange("p i n -> p n i"))
         zp_picked = keep.tile([P, S], F32, name="zp_picked")
-        for b in range(2):
-            nc.scalar.copy(zp_picked[:, b * BANK : (b + 1) * BANK], spread[b][:].rearrange("p i j -> p (i j)"))
+        nc.scalar.activation(zp_picked[:], zp_table[:].indirect(offsets[:]), ACT.Copy)
 
-        nc.vector.tensor_copy(grouped[:, :DIRECT, 0], planes[0][:].indirect(entries(0, DIRECT)))
-        nc.vector.tensor_copy(low_rows[:, 0, :VECTOR_ROWS], planes[0][:].indirect(entries(DIRECT, DIRECT + VECTOR_ROWS)))
-        nc.vector.tensor_copy(grouped[:, :DIRECT, 1], planes[1][:].indirect(entries(0, DIRECT)))
-        nc.scalar.activation(low_rows[:, 1, :], planes[1][:].indirect(entries(DIRECT, S)), ACT.Copy)
-        nc.gpsimd.tensor_scalar(grouped[:, DIRECT:, 0:2], weave_source(low_rows[:]), 1.0, 0.0, ALU.mult, ALU.add)
+        low_rows = reused.tile([P, 2, WOVEN], BF16, name="low_rows", offset=0)
+        high_rows = reused.tile([P, 2, WOVEN], BF16, name="high_rows", offset=4 * WOVEN)
+        for t in (0, 1):
+            direct(t, 0, LOW_DIRECT)
+            to_row(low_rows, t, LOW_DIRECT, S)
+        nc.gpsimd.tensor_scalar(*weave_views(low_rows, 0, LOW_DIRECT, S), 1.0, 0.0, ALU.mult, ALU.add)
 
-        early_rows = reused.tile([P, 2, EARLY], BF16, name="early_rows", offset=0)
-        late_rows = reused.tile([P, 2, S - LATE], BF16, name="late_rows", offset=LATE_ROWS_AT)
-        nc.vector.tensor_copy(grouped[:, :DIRECT, 2], planes[2][:].indirect(entries(0, DIRECT)))
-        nc.scalar.activation(early_rows[:, 0, :], planes[2][:].indirect(entries(DIRECT, LATE)), ACT.Copy)
-        nc.scalar.activation(late_rows[:, 0, :], planes[2][:].indirect(entries(LATE, S)), ACT.Copy)
+        direct(2, 0, DIRECT)
+        to_row(high_rows, 2, DIRECT, S)
 
-        for lo, hi in ((0, CHUNK), (CHUNK, DIRECT)):
-            nc.vector.tensor_copy(grouped[:, lo:hi, 3], planes[3][:].indirect(entries(lo, hi)))
-        nc.scalar.activation(early_rows[:, 1, :], planes[3][:].indirect(entries(DIRECT, LATE)), ACT.Copy)
-        nc.scalar.activation(late_rows[:, 1, :], planes[3][:].indirect(entries(LATE, S)), ACT.Copy)
-        nc.gpsimd.tensor_scalar(grouped[:, DIRECT:LATE, 2:4], weave_source(early_rows[:]), 1.0, 0.0, ALU.mult, ALU.add)
-        nc.scalar.copy(grouped[:, LATE:, 2:4], weave_source(late_rows[:]))
+        for lo in range(0, DIRECT, CHUNK):
+            direct(3, lo, lo + CHUNK)
+        for lo, hi in (POOL_RUN, *SCALAR_RUNS):
+            to_row(high_rows, 3, lo, hi)
+        nc.gpsimd.tensor_scalar(*weave_views(high_rows, 2, *POOL_RUN), 1.0, 0.0, ALU.mult, ALU.add)
+        for lo, hi in SCALAR_RUNS:
+            nc.scalar.copy(*weave_views(high_rows, 2, lo, hi))
 
-        negated = reused.tile([P, S], F32, name="negated", offset=LATE_ROWS_AT)
-        sums = []
-        for c in range(CHUNKS):
+        negated = reused.tile([P, S], F32, name="negated", offset=4 * WOVEN)
+
+        sums = {}
+        for c in CHUNK_ORDER:
             codes = keep.tile([P, CHUNK], U32, name=f"codes{c}", align_bytes=64)
             scales = keep.tile([P, CHUNK], U8, name=f"scales{c}", align_bytes=64)
             nc.vector.quantize_mx(
@@ -148,9 +136,9 @@ def tile_picked_zeropt_gelu_l_kernel(tc, xT, zp, csum, w1_words, w1_scales, offs
                 start=True,
                 stop=True,
             )
-            sums.append(acc)
+            sums[c] = acc
 
-        for c in range(CHUNKS):
+        for c in CHUNK_ORDER:
             chunk = slice(c * CHUNK, (c + 1) * CHUNK)
             nc.vector.scalar_tensor_tensor(
                 negated[:, chunk], zp_picked[:, chunk], csum_col[:], sums[c][:], ALU.mult, ALU.subtract

@@ -26,9 +26,11 @@ ZP_COLS = T // P
 DIRECT = 512
 WOVEN = S - DIRECT
 POOL_RUN = (S - 192, S)
-SCALAR_RUNS = ((672, 832), (512, 672))
-LOW_DIRECT = 704
+SCALAR_RUNS = ((640, 832), (512, 640))
+HELPED = 768
 CHUNK_ORDER = (0, 1, 3, 2)
+HALF = CHUNK // 2
+PIECES = {0: ((0, HALF), (HALF, CHUNK)), 1: ((0, CHUNK),), 3: ((0, CHUNK),), 2: ((HALF, CHUNK), (0, HALF))}
 
 
 def tile_picked_zeropt_gelu_l_kernel(tc, xT, zp, csum, w1_words, w1_scales, offs, out):
@@ -98,11 +100,14 @@ def tile_picked_zeropt_gelu_l_kernel(tc, xT, zp, csum, w1_words, w1_scales, offs
         nc.scalar.activation(zp_picked[:], zp_table[:].indirect(offsets[:]), ACT.Copy)
 
         low_rows = reused.tile([P, 2, WOVEN], BF16, name="low_rows", offset=0)
+        helped_rows = keep.tile([P, 2, HELPED - DIRECT], BF16, name="helped_rows")
         high_rows = reused.tile([P, 2, WOVEN], BF16, name="high_rows", offset=4 * WOVEN)
         for t in (0, 1):
-            direct(t, 0, LOW_DIRECT)
-            to_row(low_rows, t, LOW_DIRECT, S)
-        nc.gpsimd.tensor_scalar(*weave_views(low_rows, 0, LOW_DIRECT, S), 1.0, 0.0, ALU.mult, ALU.add)
+            nc.vector.tensor_copy(helped_rows[:, t, :], planes[t][:].indirect(entries(DIRECT, HELPED)))
+            direct(t, 0, DIRECT)
+            to_row(low_rows, t, HELPED, S)
+        nc.gpsimd.tensor_scalar(*weave_views(helped_rows, 0, DIRECT, HELPED), 1.0, 0.0, ALU.mult, ALU.add)
+        nc.gpsimd.tensor_scalar(*weave_views(low_rows, 0, HELPED, S), 1.0, 0.0, ALU.mult, ALU.add)
 
         direct(2, 0, DIRECT)
         to_row(high_rows, 2, DIRECT, S)
@@ -121,21 +126,22 @@ def tile_picked_zeropt_gelu_l_kernel(tc, xT, zp, csum, w1_words, w1_scales, offs
         for c in CHUNK_ORDER:
             codes = keep.tile([P, CHUNK], U32, name=f"codes{c}", align_bytes=64)
             scales = keep.tile([P, CHUNK], U8, name=f"scales{c}", align_bytes=64)
-            nc.vector.quantize_mx(
-                out=codes[:].bitcast(FP8X4),
-                scales=scales[:],
-                in_=grouped[:, c * CHUNK : (c + 1) * CHUNK].rearrange("p j t -> p (j t)"),
-            )
             acc = psum.tile([P, CHUNK], F32, name=f"acc{c}")
-            nc.tensor.matmul_mx(
-                out=acc[:],
-                lhsT=w_words[:].bitcast(FP4X4),
-                lhsT_scale=w_scales[:],
-                rhs=codes[:].bitcast(FP8X4),
-                rhs_scale=scales[:],
-                start=True,
-                stop=True,
-            )
+            for lo, hi in PIECES[c]:
+                nc.vector.quantize_mx(
+                    out=codes[:, lo:hi].bitcast(FP8X4),
+                    scales=scales[:, lo:hi],
+                    in_=grouped[:, c * CHUNK + lo : c * CHUNK + hi].rearrange("p j t -> p (j t)"),
+                )
+                nc.tensor.matmul_mx(
+                    out=acc[:, lo:hi],
+                    lhsT=w_words[:].bitcast(FP4X4),
+                    lhsT_scale=w_scales[:],
+                    rhs=codes[:, lo:hi].bitcast(FP8X4),
+                    rhs_scale=scales[:, lo:hi],
+                    start=True,
+                    stop=True,
+                )
             sums[c] = acc
 
         for c in CHUNK_ORDER:

@@ -30,7 +30,7 @@ SCALAR_RUNS = ((640, 832), (512, 640))
 HELPED = 768
 CHUNK_ORDER = (0, 1, 3, 2)
 HALF = CHUNK // 2
-PIECES = {0: ((0, HALF), (HALF, CHUNK)), 1: ((0, CHUNK),), 3: ((0, CHUNK),), 2: ((HALF, CHUNK), (0, HALF))}
+PIECES = {c: ((HALF, CHUNK), (0, HALF)) if c >= 2 else ((0, HALF), (HALF, CHUNK)) for c in CHUNK_ORDER}
 
 
 def tile_picked_zeropt_gelu_l_kernel(tc, xT, zp, csum, w1_words, w1_scales, offs, out):

@@ -146,9 +146,11 @@ def tile_picked_zeropt_gelu_l_kernel(tc, xT, zp, csum, w1_words, w1_scales, offs
 
         for c in CHUNK_ORDER:
             chunk = slice(c * CHUNK, (c + 1) * CHUNK)
-            nc.vector.scalar_tensor_tensor(
-                negated[:, chunk], zp_picked[:, chunk], csum_col[:], sums[c][:], ALU.mult, ALU.subtract
-            )
             result = keep.tile([P, CHUNK], F32, name=f"result{c}")
-            nc.scalar.activation(result[:], negated[:, chunk], ACT.Gelu_apprx_tanh, scale=-1.0)
+            for lo, hi in PIECES[c]:
+                piece = slice(c * CHUNK + lo, c * CHUNK + hi)
+                nc.vector.scalar_tensor_tensor(
+                    negated[:, piece], zp_picked[:, piece], csum_col[:], sums[c][:, lo:hi], ALU.mult, ALU.subtract
+                )
+                nc.scalar.activation(result[:, lo:hi], negated[:, piece], ACT.Gelu_apprx_tanh, scale=-1.0)
             nc.sync.dma_start(out[:, chunk], result[:])

@@ -25,12 +25,13 @@ ZP_COLS = T // P
 
 DIRECT = 512
 WOVEN = S - DIRECT
-POOL_RUN = (S - 192, S)
-SCALAR_RUNS = ((640, 832), (512, 640))
+POOL_RUNS = ((928, S), (800, 928))
+SCALAR_RUNS = ((640, 800), (512, 640))
 HELPED = 768
 CHUNK_ORDER = (0, 1, 3, 2)
 HALF = CHUNK // 2
 PIECES = {c: ((HALF, CHUNK), (0, HALF)) if c >= 2 else ((0, HALF), (HALF, CHUNK)) for c in CHUNK_ORDER}
+WHOLE = (0, 1)
 
 
 def tile_picked_zeropt_gelu_l_kernel(tc, xT, zp, csum, w1_words, w1_scales, offs, out):
@@ -114,9 +115,10 @@ def tile_picked_zeropt_gelu_l_kernel(tc, xT, zp, csum, w1_words, w1_scales, offs
 
         for lo in range(0, DIRECT, CHUNK):
             direct(3, lo, lo + CHUNK)
-        for lo, hi in (POOL_RUN, *SCALAR_RUNS):
+        for lo, hi in (*POOL_RUNS, *SCALAR_RUNS):
             to_row(high_rows, 3, lo, hi)
-        nc.gpsimd.tensor_scalar(*weave_views(high_rows, 2, *POOL_RUN), 1.0, 0.0, ALU.mult, ALU.add)
+        for lo, hi in POOL_RUNS:
+            nc.gpsimd.tensor_scalar(*weave_views(high_rows, 2, lo, hi), 1.0, 0.0, ALU.mult, ALU.add)
         for lo, hi in SCALAR_RUNS:
             nc.scalar.copy(*weave_views(high_rows, 2, lo, hi))
 
@@ -127,12 +129,19 @@ def tile_picked_zeropt_gelu_l_kernel(tc, xT, zp, csum, w1_words, w1_scales, offs
             codes = keep.tile([P, CHUNK], U32, name=f"codes{c}", align_bytes=64)
             scales = keep.tile([P, CHUNK], U8, name=f"scales{c}", align_bytes=64)
             acc = psum.tile([P, CHUNK], F32, name=f"acc{c}")
-            for lo, hi in PIECES[c]:
+
+            def quantise(lo, hi):
                 nc.vector.quantize_mx(
                     out=codes[:, lo:hi].bitcast(FP8X4),
                     scales=scales[:, lo:hi],
                     in_=grouped[:, c * CHUNK + lo : c * CHUNK + hi].rearrange("p j t -> p (j t)"),
                 )
+
+            if c in WHOLE:
+                quantise(0, CHUNK)
+            for lo, hi in PIECES[c]:
+                if c not in WHOLE:
+                    quantise(lo, hi)
                 nc.tensor.matmul_mx(
                     out=acc[:, lo:hi],
                     lhsT=w_words[:].bitcast(FP4X4),

from contextlib import ExitStack

import concourse.mybir as mybir
from concourse.masks import make_identity

K, T, S, N = 512, 2048, 1024, 128
P = 128
FLOPS = 2 * K * S * N

F32 = mybir.dt.float32
BF16 = mybir.dt.bfloat16
U32 = mybir.dt.uint32
I32 = mybir.dt.int32
U16 = mybir.dt.uint16
U8 = mybir.dt.uint8
FP8X4 = mybir.dt.float8_e4m3fn_x4
FP4X4 = mybir.dt.float4_e2m1fn_x4
ACT = mybir.ActivationFunctionType
ALU = mybir.AluOpType

CHUNK = 256
CHUNKS = S // CHUNK
LIST_ROWS = 16
ZP_COLS = T // P

DIRECT = 512
WOVEN = S - DIRECT
POOL_RUNS = ((928, S), (800, 928))
SCALAR_RUNS = ((640, 800), (512, 640))
HELPED = 768
CHUNK_ORDER = (0, 1, 3, 2)
HALF = CHUNK // 2
PIECES = {c: ((HALF, CHUNK), (0, HALF)) if c >= 2 else ((0, HALF), (HALF, CHUNK)) for c in CHUNK_ORDER}
WHOLE = (0, 1)


def tile_picked_zeropt_gelu_l_kernel(tc, xT, zp, csum, w1_words, w1_scales, offs, out):
    nc = tc.nc
    with ExitStack() as ctx:
        keep = ctx.enter_context(tc.tile_pool(name="keep", bufs=1))
        reused = ctx.enter_context(tc.tile_pool(name="reused", bufs=1))
        psum = ctx.enter_context(tc.psum_pool(name="psum", bufs=1))

        offsets = keep.tile([P, S // LIST_ROWS], U16, name="offsets")

        def entries(lo, hi):
            return offsets[:, lo // LIST_ROWS : hi // LIST_ROWS]

        warm = keep.tile([P, 2], F32, name="warm")
        nc.vector.memset(warm[:, 0:1], 0.0)
        nc.scalar.activation(warm[:, 1:2], warm[:, 0:1], ACT.Gelu_apprx_tanh)

        w_scales = keep.tile([P, N], U8, name="w_scales", align_bytes=64)
        nc.vector.memset(w_scales[:].bitcast(I32), 0)

        rows = xT.rearrange("(p t) c -> p t c", t=4)
        planes = [keep.tile([P, T], F32, name=f"plane{t}") for t in range(4)]
        zp_dealt = keep.tile([P, ZP_COLS], F32, name="zp_dealt")
        nc.sync.dma_start(zp_dealt[:], zp[0].rearrange("(p i) -> p i", i=ZP_COLS))
        nc.sync.dma_start(planes[0][:], rows[:, 0, :])
        nc.sync.dma_start(offsets[:], offs)
        for t in range(1, 4):
            nc.sync.dma_start(planes[t][:], rows[:, t, :])

        w_words = keep.tile([P, 2 * N], U8, name="w_words", align_bytes=64)
        csum_col = keep.tile([P, 1], F32, name="csum_col")
        nc.sync.dma_start(w_words[:].bitcast(I32), w1_words[0].bitcast(I32))
        for q in range(4):
            nc.sync.dma_start(
                w_scales[32 * q : 32 * q + 4, :].bitcast(I32),
                w1_scales[0, 4 * q : 4 * q + 4, :].bitcast(I32),
            )
        nc.sync.dma_start(csum_col[:], csum)

        identity = keep.tile([P, P], F32, name="identity")
        make_identity(nc, identity[:])

        grouped = keep.tile([P, S, 4], BF16, name="grouped", align_bytes=64)

        def direct(t, lo, hi):
            nc.vector.tensor_copy(grouped[:, lo:hi, t], planes[t][:].indirect(entries(lo, hi)))

        def to_row(two_rows, t, lo, hi):
            nc.scalar.activation(
                two_rows[:, t % 2, lo - DIRECT : hi - DIRECT], planes[t][:].indirect(entries(lo, hi)), ACT.Copy
            )

        def weave_views(two_rows, first_t, lo, hi):
            source = two_rows[:, :, lo - DIRECT : hi - DIRECT].rearrange("p e j -> p j e")
            return grouped[:, lo:hi, first_t : first_t + 2], source

        zp_table = reused.tile([P, T], F32, name="zp_table", offset=0)
        table_by_bank = zp_table[:].rearrange("p (n b i) -> p b n i", b=4, i=4)
        for b in range(4):
            bank = psum.tile([P, 4, P], F32, name=f"spread{b}")
            for i in range(4):
                col = 4 * b + i
                nc.tensor.transpose(bank[:, i, :], zp_dealt[:, col : col + 1].to_broadcast([P, P]), identity[:])
            nc.scalar.copy(table_by_bank[:, b], bank[:].rearrange("p i n -> p n i"))
        zp_picked = keep.tile([P, S], F32, name="zp_picked")
        nc.scalar.activation(zp_picked[:], zp_table[:].indirect(offsets[:]), ACT.Copy)

        low_rows = reused.tile([P, 2, WOVEN], BF16, name="low_rows", offset=0)
        helped_rows = keep.tile([P, 2, HELPED - DIRECT], BF16, name="helped_rows")
        high_rows = reused.tile([P, 2, WOVEN], BF16, name="high_rows", offset=4 * WOVEN)
        for t in (0, 1):
            nc.vector.tensor_copy(helped_rows[:, t, :], planes[t][:].indirect(entries(DIRECT, HELPED)))
            direct(t, 0, DIRECT)
            to_row(low_rows, t, HELPED, S)
        nc.gpsimd.tensor_scalar(*weave_views(helped_rows, 0, DIRECT, HELPED), 1.0, 0.0, ALU.mult, ALU.add)
        nc.gpsimd.tensor_scalar(*weave_views(low_rows, 0, HELPED, S), 1.0, 0.0, ALU.mult, ALU.add)

        direct(2, 0, DIRECT)
        to_row(high_rows, 2, DIRECT, S)

        for lo in range(0, DIRECT, CHUNK):
            direct(3, lo, lo + CHUNK)
        for lo, hi in (*POOL_RUNS, *SCALAR_RUNS):
            to_row(high_rows, 3, lo, hi)
        for lo, hi in POOL_RUNS:
            nc.gpsimd.tensor_scalar(*weave_views(high_rows, 2, lo, hi), 1.0, 0.0, ALU.mult, ALU.add)
        for lo, hi in SCALAR_RUNS:
            nc.scalar.copy(*weave_views(high_rows, 2, lo, hi))

        negated = reused.tile([P, S], F32, name="negated", offset=4 * WOVEN)

        sums = {}
        for c in CHUNK_ORDER:
            codes = keep.tile([P, CHUNK], U32, name=f"codes{c}", align_bytes=64)
            scales = keep.tile([P, CHUNK], U8, name=f"scales{c}", align_bytes=64)
            acc = psum.tile([P, CHUNK], F32, name=f"acc{c}")

            def quantise(lo, hi):
                nc.vector.quantize_mx(
                    out=codes[:, lo:hi].bitcast(FP8X4),
                    scales=scales[:, lo:hi],
                    in_=grouped[:, c * CHUNK + lo : c * CHUNK + hi].rearrange("p j t -> p (j t)"),
                )

            if c in WHOLE:
                quantise(0, CHUNK)
            for lo, hi in PIECES[c]:
                if c not in WHOLE:
                    quantise(lo, hi)
                nc.tensor.matmul_mx(
                    out=acc[:, lo:hi],
                    lhsT=w_words[:].bitcast(FP4X4),
                    lhsT_scale=w_scales[:],
                    rhs=codes[:, lo:hi].bitcast(FP8X4),
                    rhs_scale=scales[:, lo:hi],
                    start=True,
                    stop=True,
                )
            sums[c] = acc

        for c in CHUNK_ORDER:
            chunk = slice(c * CHUNK, (c + 1) * CHUNK)
            result = keep.tile([P, CHUNK], F32, name=f"result{c}")
            for lo, hi in PIECES[c]:
                piece = slice(c * CHUNK + lo, c * CHUNK + hi)
                nc.vector.scalar_tensor_tensor(
                    negated[:, piece], zp_picked[:, piece], csum_col[:], sums[c][:, lo:hi], ALU.mult, ALU.subtract
                )
                nc.scalar.activation(result[:, lo:hi], negated[:, piece], ACT.Gelu_apprx_tanh, scale=-1.0)
            nc.sync.dma_start(out[:, chunk], result[:])
